import numpy as np
import ml_dtypes


def mxq(x, axis, fmt="e4m3"):
    dtype, down = {"e4m3": (ml_dtypes.float8_e4m3fn, 7), "e5m2": (ml_dtypes.float8_e5m2, 14)}[fmt]
    v = np.moveaxis(np.asarray(x, np.float32).astype(ml_dtypes.bfloat16).astype(np.float64), axis, -1)
    blocks = v.reshape(v.shape[:-1] + (-1, 32))
    amax = np.abs(blocks).max(-1, keepdims=True)
    byte = np.maximum(np.where(amax > 0, np.frexp(amax)[1] - 1 + 127, 0) - down, 1)
    scale = np.exp2(byte - 127.0)
    codes = (blocks / scale).astype(np.float32).astype(dtype).astype(np.float64)
    return np.moveaxis((codes * scale).reshape(v.shape), -1, axis)


WIDE = False


def mx_kscale(k):
    if not WIDE:
        return np.ones(k)
    levels = np.array([10, -10, 5, -5, 0])
    if k % 512:
        return np.exp2(np.random.permutation(np.resize(levels, k // 32))).repeat(32)
    a = np.empty((k // 512, 16))
    for p in range(k // 512):
        a[p, :8] = np.random.permutation(np.resize(levels, 8))
        for g in range(8):
            far = levels[np.abs(levels - a[p, g]) >= 10]
            a[p, g + 8] = far[np.random.randint(len(far))]
    return np.exp2(a.ravel()).repeat(32)


def f64(x):
    return np.asarray(x).astype(np.float64)


def striped(idx):
    return np.tile(idx.reshape(-1, 16).T, (8, 1)).astype(np.uint16)


def unstriped(offs):
    return offs[:16].T.reshape(-1).astype(np.int64)


def pack_weight(w):
    k, n = w.shape
    w = f64(np.asarray(w, np.float32).astype(ml_dtypes.bfloat16)).reshape(k // 32, 32, n)
    amax = np.abs(w).max(1)
    byte = np.clip(np.where(amax > 0, np.frexp(amax)[1] - 1 + 127 - 7, 1), 1, 254)
    scaled = (w * np.exp2(127.0 - byte)[:, None, :]).reshape(k, n).astype(np.float32)
    words = np.ascontiguousarray(scaled.reshape(k // 512, 128, 4, n).transpose(0, 1, 3, 2)).astype(ml_dtypes.float8_e4m3fn).view(np.uint8)
    return words, np.ascontiguousarray(byte.astype(np.uint8).reshape(k // 512, 16, n))


def unpack_weight(words, scales):
    g, p, n, _ = words.shape
    vals = np.ascontiguousarray(words).view(ml_dtypes.float8_e4m3fn).astype(np.float64) * np.repeat(np.exp2(scales.astype(np.float64) - 127.0), 8, axis=1)[..., None]
    return vals.transpose(0, 1, 3, 2).reshape(g * 512, n)

def planes(y):
    n, m = y.shape
    v = y.astype(np.float32).astype(ml_dtypes.bfloat16).astype(np.float64).reshape(n // 32, 32, m)
    top = np.abs(v).max(1)
    byte = np.clip(np.where(top > 0, np.frexp(top)[1] - 1 + 127 - 7, 1), 1, 254)
    codes = (v * np.exp2(127.0 - byte)[:, None, :]).reshape(n, m).astype(np.float32).astype(ml_dtypes.float8_e4m3fn).view(np.uint8)
    words = codes.reshape(n // 512, 128, 4, m).transpose(0, 1, 3, 2)
    return np.ascontiguousarray(words), np.ascontiguousarray(byte.astype(np.uint8).reshape(n // 512, 16, m))


K, T, S, N, U = 512, 2048, 512, 512, 1024


def setup_inputs():
    n = np.random.standard_normal
    s = mx_kscale(K)[:, None]
    packed_xT = pack_weight(n((K, T)) * s)
    return {
        "x_words": packed_xT[0],
        "x_scales": packed_xT[1],
        "w1": (n((K, N)) / np.sqrt(K) / s).astype(np.float32),
        "gamma": np.random.uniform(0.5, 1.5, (N, U)).astype(np.float32),
        "beta": (0.5 * n((N, U))).astype(np.float32),
        "offs": striped(np.random.permutation(T)[:S]),
        "cls": striped(np.random.randint(0, U, S)),
    }


def reference(x_words, x_scales, w1, gamma, beta, offs, cls):
    xq = unpack_weight(x_words, x_scales)[:, unstriped(offs)]
    y = mxq(f64(w1), 0, "e4m3").T @ xq
    g = f64(gamma)[:, unstriped(cls)]
    s = f64(beta)[:, unstriped(cls)]
    out_0 = y * g + s
    return (out_0,) + planes(out_0)

@@ -1,0 +1,134 @@
+from contextlib import ExitStack
+
+import concourse.mybir as mybir
+
+K, T, S, N, U = 512, 2048, 512, 512, 1024
+FLOPS = 2 * K * N * S
+
+F32 = mybir.dt.float32
+BF16 = mybir.dt.bfloat16
+I32 = mybir.dt.int32
+U32 = mybir.dt.uint32
+U16 = mybir.dt.uint16
+U8 = mybir.dt.uint8
+FP8X4 = mybir.dt.float8_e4m3fn_x4
+MULT = mybir.AluOpType.mult
+ADD = mybir.AluOpType.add
+
+P = 128
+PACK = 4
+HALF = S // 2
+
+
+def tile_picked_cbn_none_po_kernel(tc, x_words, x_scales, w1, gamma, beta, offs, cls, out_0, out_1, out_2):
+    nc = tc.nc
+    with ExitStack() as ctx:
+        keep = ctx.enter_context(tc.tile_pool(name="keep", bufs=1))
+        psum = ctx.enter_context(tc.psum_pool(name="psum", bufs=1))
+
+        def entries(lst, lo, hi):
+            return lst[:, lo // 16 : hi // 16]
+
+        offs_t = keep.tile([P, S // 16], U16, name="offs_t")
+        cls_t = keep.tile([P, S // 16], U16, name="cls_t")
+        xw = keep.tile([P, T], I32, name="xw", align_bytes=64)
+        xs = keep.tile([P, T], U8, name="xs", align_bytes=64)
+        w_raw = [keep.tile([P, PACK, N // 2], F32, name=f"w_raw{h}", align_bytes=64) for h in range(2)]
+        g_tab = [keep.tile([P, U], F32, name=f"g_tab{t}", align_bytes=64) for t in range(PACK)]
+        b_tab = [keep.tile([P, U], F32, name=f"b_tab{t}", align_bytes=64) for t in range(PACK)]
+
+        nc.vector.memset(xs[:].bitcast(I32), 0)
+
+        w_rows = w1.rearrange("(p j) c -> p j c", j=PACK)
+        g_rows = gamma.rearrange("(p t) u -> p t u", t=PACK)
+        b_rows = beta.rearrange("(p t) u -> p t u", t=PACK)
+        o_rows = out_0.rearrange("(p t) s -> p t s", t=PACK)
+
+        nc.sync.dma_start(out=w_raw[0][:], in_=w_rows[:, :, 0 : N // 2])
+        nc.sync.dma_start(out=offs_t[:], in_=offs)
+        nc.sync.dma_start(out=w_raw[1][:], in_=w_rows[:, :, N // 2 : N])
+        for q in range(4):
+            nc.scalar.dma_start(out=xs[32 * q : 32 * q + 4, :].bitcast(I32), in_=x_scales[0, 4 * q : 4 * q + 4, :].bitcast(I32))
+        nc.sync.dma_start(out=xw[:], in_=x_words[0].rearrange("p c r -> p (c r)").bitcast(I32))
+        nc.sync.dma_start(out=cls_t[:], in_=cls)
+        for t in range(PACK):
+            nc.sync.dma_start(out=g_tab[t][:], in_=g_rows[:, t, :])
+            nc.sync.dma_start(out=b_tab[t][:], in_=b_rows[:, t, :])
+
+        w_bf = keep.tile([P, PACK, P, PACK], BF16, name="w_bf", align_bytes=64)
+        w_dst = w_bf[:].rearrange("p t m j -> p m j t")
+        nc.scalar.copy(out=w_dst[:, 0 : P // 2], in_=w_raw[0][:].rearrange("p j (m t) -> p m j t", t=PACK))
+
+        xg_s = keep.tile([P, S], U8, name="xg_s", align_bytes=64)
+        nc.vector.tensor_copy(out=xg_s[:], in_=xs[:].indirect(offs_t[:]))
+
+        nc.vector.tensor_copy(out=w_dst[:, P // 2 : P], in_=w_raw[1][:].rearrange("p j (m t) -> p m j t", t=PACK))
+        w_codes = keep.tile([P, N], U32, name="w_codes", align_bytes=64)
+        w_sc = keep.tile([P, N], U8, name="w_sc", align_bytes=64)
+        nc.vector.quantize_mx(out=w_codes[:].bitcast(FP8X4), scales=w_sc[:], in_=w_bf[:].rearrange("p t m j -> p (t m j)"))
+
+        xg_w = keep.tile([P, S], U32, name="xg_w", align_bytes=64)
+        for lo in (0, HALF):
+            nc.vector.tensor_copy(out=xg_w[:, lo : lo + HALF], in_=xw[:].bitcast(U32).indirect(entries(offs_t, lo, lo + HALF)))
+
+        y = keep.tile([P, PACK, S], F32, name="y", align_bytes=64)
+        yg = keep.tile([P, PACK, S], F32, name="yg", align_bytes=64)
+        res = keep.tile([P, PACK, S], F32, name="res", align_bytes=64)
+
+        def product(t, lo, hi):
+            acc = psum.tile([P, hi - lo], F32, name=f"acc{t}_{lo}")
+            nc.tensor.matmul_mx(
+                out=acc[:],
+                lhsT=w_codes[:, t * P : (t + 1) * P].bitcast(FP8X4),
+                lhsT_scale=w_sc[:, t * P : (t + 1) * P],
+                rhs=xg_w[:, lo:hi].bitcast(FP8X4),
+                rhs_scale=xg_s[:, lo:hi],
+                start=True,
+                stop=True,
+            )
+            nc.scalar.copy(out=y[:, t, lo:hi], in_=acc[:])
+
+        def scale(t, lo, hi):
+            nc.vector.tensor_tensor(out=yg[:, t, lo:hi], in0=g_tab[t][:].indirect(entries(cls_t, lo, hi)), in1=y[:, t, lo:hi], op=MULT)
+
+        def shift(t, lo, hi):
+            nc.vector.tensor_tensor(out=res[:, t, lo:hi], in0=b_tab[t][:].indirect(entries(cls_t, lo, hi)), in1=yg[:, t, lo:hi], op=ADD)
+
+        product(0, 0, HALF)
+        product(0, HALF, S)
+        for t in range(1, PACK):
+            product(t, 0, S)
+
+        scale(0, 0, HALF)
+        scale(0, HALF, S)
+        for t in range(PACK - 1):
+            shift(t, 0, S)
+            scale(t + 1, 0, S)
+            nc.sync.dma_start(out=o_rows[:, t, :], in_=res[:, t, :])
+
+        o_bf = [keep.tile([P, HALF, PACK], BF16, name=f"o_bf{h}", align_bytes=64) for h in range(2)]
+        o_codes = keep.tile([P, S], I32, name="o_codes", align_bytes=64)
+        o_sc = keep.tile([P, S], U8, name="o_sc", align_bytes=64)
+        words_out = out_1[0].rearrange("p c r -> p (c r)").bitcast(I32)
+
+        def weave(engine_copy, h):
+            engine_copy(
+                out=o_bf[h][:].rearrange("p (c i) t -> p c t i", i=4),
+                in_=res[:, :, h * HALF : (h + 1) * HALF].rearrange("p t (c i) -> p c t i", i=4),
+            )
+
+        def pack(h):
+            cols = slice(h * HALF, (h + 1) * HALF)
+            nc.vector.quantize_mx(out=o_codes[:, cols].bitcast(FP8X4), scales=o_sc[:, cols], in_=o_bf[h][:].rearrange("p c t -> p (c t)"))
+            nc.sync.dma_start(out=words_out[:, cols], in_=o_codes[:, cols])
+
+        shift(3, 0, HALF)
+        weave(nc.scalar.copy, 0)
+        shift(3, HALF, S)
+        nc.sync.dma_start(out=o_rows[:, 3, :], in_=res[:, 3, :])
+        weave(nc.vector.tensor_copy, 1)
+        pack(0)
+        pack(1)
+        for q in range(4):
+            eng = nc.scalar if q % 2 == 0 else nc.sync
+            eng.dma_start(out=out_2[0, 4 * q : 4 * q + 4, :].bitcast(I32), in_=o_sc[32 * q : 32 * q + 4, :].bitcast(I32))

@@ -37,8 +37,6 @@ def tile_picked_cbn_none_po_kernel(tc, x_words, x_scales, w1, gamma, beta, offs,
         g_tab = [keep.tile([P, U], F32, name=f"g_tab{t}", align_bytes=64) for t in range(PACK)]
         b_tab = [keep.tile([P, U], F32, name=f"b_tab{t}", align_bytes=64) for t in range(PACK)]
 
-        nc.vector.memset(xs[:].bitcast(I32), 0)
-
         w_rows = w1.rearrange("(p j) c -> p j c", j=PACK)
         g_rows = gamma.rearrange("(p t) u -> p t u", t=PACK)
         b_rows = beta.rearrange("(p t) u -> p t u", t=PACK)
@@ -46,14 +44,13 @@ def tile_picked_cbn_none_po_kernel(tc, x_words, x_scales, w1, gamma, beta, offs,
 
         nc.sync.dma_start(out=w_raw[0][:], in_=w_rows[:, :, 0 : N // 2])
         nc.sync.dma_start(out=offs_t[:], in_=offs)
-        nc.sync.dma_start(out=w_raw[1][:], in_=w_rows[:, :, N // 2 : N])
         for q in range(4):
-            nc.scalar.dma_start(out=xs[32 * q : 32 * q + 4, :].bitcast(I32), in_=x_scales[0, 4 * q : 4 * q + 4, :].bitcast(I32))
+            nc.sync.dma_start(out=xs[32 * q : 32 * q + 32, :].bitcast(I32), in_=x_scales[0, 4 * q : 4 * q + 4, :].bitcast(I32).partition_broadcast(8))
+        nc.sync.dma_start(out=w_raw[1][:], in_=w_rows[:, :, N // 2 : N])
         nc.sync.dma_start(out=xw[:], in_=x_words[0].rearrange("p c r -> p (c r)").bitcast(I32))
         nc.sync.dma_start(out=cls_t[:], in_=cls)
-        for t in range(PACK):
-            nc.sync.dma_start(out=g_tab[t][:], in_=g_rows[:, t, :])
-            nc.sync.dma_start(out=b_tab[t][:], in_=b_rows[:, t, :])
+        for tab, rows, t in ((g_tab, g_rows, 0), (g_tab, g_rows, 1), (b_tab, b_rows, 0), (g_tab, g_rows, 2), (b_tab, b_rows, 1), (b_tab, b_rows, 2), (b_tab, b_rows, 3), (g_tab, g_rows, 3)):
+            nc.sync.dma_start(out=tab[t][:], in_=rows[:, t, :])
 
         w_bf = keep.tile([P, PACK, P, PACK], BF16, name="w_bf", align_bytes=64)
         w_dst = w_bf[:].rearrange("p t m j -> p m j t")
@@ -62,7 +59,7 @@ def tile_picked_cbn_none_po_kernel(tc, x_words, x_scales, w1, gamma, beta, offs,
         xg_s = keep.tile([P, S], U8, name="xg_s", align_bytes=64)
         nc.vector.tensor_copy(out=xg_s[:], in_=xs[:].indirect(offs_t[:]))
 
-        nc.vector.tensor_copy(out=w_dst[:, P // 2 : P], in_=w_raw[1][:].rearrange("p j (m t) -> p m j t", t=PACK))
+        nc.scalar.copy(out=w_dst[:, P // 2 : P], in_=w_raw[1][:].rearrange("p j (m t) -> p m j t", t=PACK))
         w_codes = keep.tile([P, N], U32, name="w_codes", align_bytes=64)
         w_sc = keep.tile([P, N], U8, name="w_sc", align_bytes=64)
         nc.vector.quantize_mx(out=w_codes[:].bitcast(FP8X4), scales=w_sc[:], in_=w_bf[:].rearrange("p t m j -> p (t m j)"))
@@ -86,7 +83,7 @@ def tile_picked_cbn_none_po_kernel(tc, x_words, x_scales, w1, gamma, beta, offs,
                 start=True,
                 stop=True,
             )
-            nc.scalar.copy(out=y[:, t, lo:hi], in_=acc[:])
+            return acc
 
         def scale(t, lo, hi):
             nc.vector.tensor_tensor(out=yg[:, t, lo:hi], in0=g_tab[t][:].indirect(entries(cls_t, lo, hi)), in1=y[:, t, lo:hi], op=MULT)
@@ -94,41 +91,44 @@ def tile_picked_cbn_none_po_kernel(tc, x_words, x_scales, w1, gamma, beta, offs,
         def shift(t, lo, hi):
             nc.vector.tensor_tensor(out=res[:, t, lo:hi], in0=b_tab[t][:].indirect(entries(cls_t, lo, hi)), in1=yg[:, t, lo:hi], op=ADD)
 
-        product(0, 0, HALF)
-        product(0, HALF, S)
+        acc0 = [product(0, lo, lo + HALF) for lo in (0, HALF)]
         for t in range(1, PACK):
-            product(t, 0, S)
+            nc.scalar.copy(out=y[:, t, :], in_=product(t, 0, S)[:])
 
-        scale(0, 0, HALF)
-        scale(0, HALF, S)
+        nc.vector.tensor_copy(out=y[:, 0, :], in_=g_tab[0][:].indirect(cls_t[:]))
+        for h in range(2):
+            cols = slice(h * HALF, (h + 1) * HALF)
+            nc.vector.tensor_tensor(out=yg[:, 0, cols], in0=acc0[h][:], in1=y[:, 0, cols], op=MULT)
         for t in range(PACK - 1):
+            if t + 1 < PACK - 1:
+                scale(t + 1, 0, S)
             shift(t, 0, S)
-            scale(t + 1, 0, S)
             nc.sync.dma_start(out=o_rows[:, t, :], in_=res[:, t, :])
 
-        o_bf = [keep.tile([P, HALF, PACK], BF16, name=f"o_bf{h}", align_bytes=64) for h in range(2)]
+        o_bf = keep.tile([P, S, PACK], BF16, name="o_bf", align_bytes=64)
         o_codes = keep.tile([P, S], I32, name="o_codes", align_bytes=64)
         o_sc = keep.tile([P, S], U8, name="o_sc", align_bytes=64)
         words_out = out_1[0].rearrange("p c r -> p (c r)").bitcast(I32)
 
-        def weave(engine_copy, h):
-            engine_copy(
-                out=o_bf[h][:].rearrange("p (c i) t -> p c t i", i=4),
-                in_=res[:, :, h * HALF : (h + 1) * HALF].rearrange("p t (c i) -> p c t i", i=4),
+        def weave(engine_copy, t0, lo, hi):
+            engine_copy(out=o_bf[:, lo:hi, t0 : t0 + 2], in_=res[:, t0 : t0 + 2, lo:hi].rearrange("p t c -> p c t"))
+
+        def pack(lo, hi):
+            nc.vector.quantize_mx(
+                out=o_codes[:, lo:hi].bitcast(FP8X4), scales=o_sc[:, lo:hi], in_=o_bf[:].rearrange("p c t -> p (c t)")[:, PACK * lo : PACK * hi]
             )
+            nc.sync.dma_start(out=words_out[:, lo:hi], in_=o_codes[:, lo:hi])
 
-        def pack(h):
-            cols = slice(h * HALF, (h + 1) * HALF)
-            nc.vector.quantize_mx(out=o_codes[:, cols].bitcast(FP8X4), scales=o_sc[:, cols], in_=o_bf[h][:].rearrange("p c t -> p (c t)"))
-            nc.sync.dma_start(out=words_out[:, cols], in_=o_codes[:, cols])
-
+        weave(nc.scalar.copy, 0, 0, S)
+        scale(3, 0, HALF)
+        scale(3, HALF, S)
         shift(3, 0, HALF)
-        weave(nc.scalar.copy, 0)
+        weave(nc.scalar.copy, 2, 0, HALF)
         shift(3, HALF, S)
         nc.sync.dma_start(out=o_rows[:, 3, :], in_=res[:, 3, :])
-        weave(nc.vector.tensor_copy, 1)
-        pack(0)
-        pack(1)
+        weave(nc.vector.tensor_copy, 2, HALF, S)
+        pack(0, HALF)
+        pack(HALF, S)
         for q in range(4):
             eng = nc.scalar if q % 2 == 0 else nc.sync
             eng.dma_start(out=out_2[0, 4 * q : 4 * q + 4, :].bitcast(I32), in_=o_sc[32 * q : 32 * q + 4, :].bitcast(I32))

@@ -33,7 +33,8 @@ def tile_picked_cbn_none_po_kernel(tc, x_words, x_scales, w1, gamma, beta, offs,
         cls_t = keep.tile([P, S // 16], U16, name="cls_t")
         xw = keep.tile([P, T], I32, name="xw", align_bytes=64)
         xs = keep.tile([P, T], U8, name="xs", align_bytes=64)
-        w_raw = [keep.tile([P, PACK, N // 2], F32, name=f"w_raw{h}", align_bytes=64) for h in range(2)]
+        xs_rows = keep.tile([P, T // 4], I32, name="xs_rows", align_bytes=64)
+        w_raw = keep.tile([P, PACK, N], F32, name="w_raw", align_bytes=64)
         g_tab = [keep.tile([P, U], F32, name=f"g_tab{t}", align_bytes=64) for t in range(PACK)]
         b_tab = [keep.tile([P, U], F32, name=f"b_tab{t}", align_bytes=64) for t in range(PACK)]
 
@@ -42,29 +43,32 @@ def tile_picked_cbn_none_po_kernel(tc, x_words, x_scales, w1, gamma, beta, offs,
         b_rows = beta.rearrange("(p t) u -> p t u", t=PACK)
         o_rows = out_0.rearrange("(p t) s -> p t s", t=PACK)
 
-        nc.sync.dma_start(out=w_raw[0][:], in_=w_rows[:, :, 0 : N // 2])
+        nc.vector.memset(xs[:].bitcast(I32), 0)
+        for r in range(4):
+            nc.scalar.dma_start(out=xs_rows[r:P:32, :], in_=x_scales[0, r:16:4, :].bitcast(I32))
         nc.sync.dma_start(out=offs_t[:], in_=offs)
-        for q in range(4):
-            nc.sync.dma_start(out=xs[32 * q : 32 * q + 32, :].bitcast(I32), in_=x_scales[0, 4 * q : 4 * q + 4, :].bitcast(I32).partition_broadcast(8))
-        nc.sync.dma_start(out=w_raw[1][:], in_=w_rows[:, :, N // 2 : N])
+        nc.sync.dma_start(out=w_raw[:], in_=w_rows)
         nc.sync.dma_start(out=xw[:], in_=x_words[0].rearrange("p c r -> p (c r)").bitcast(I32))
         nc.sync.dma_start(out=cls_t[:], in_=cls)
-        for tab, rows, t in ((g_tab, g_rows, 0), (g_tab, g_rows, 1), (b_tab, b_rows, 0), (g_tab, g_rows, 2), (b_tab, b_rows, 1), (b_tab, b_rows, 2), (b_tab, b_rows, 3), (g_tab, g_rows, 3)):
+        for tab, rows, t in ((g_tab, g_rows, 0), (g_tab, g_rows, 1), (b_tab, b_rows, 0), (g_tab, g_rows, 2), (b_tab, b_rows, 1), (g_tab, g_rows, 3), (b_tab, b_rows, 2), (b_tab, b_rows, 3)):
             nc.sync.dma_start(out=tab[t][:], in_=rows[:, t, :])
 
-        w_bf = keep.tile([P, PACK, P, PACK], BF16, name="w_bf", align_bytes=64)
+        w_bf = keep.tile([P, PACK, P, PACK], BF16, name="w_bf", tag="w_bf_then_xg_w", align_bytes=64)
         w_dst = w_bf[:].rearrange("p t m j -> p m j t")
-        nc.scalar.copy(out=w_dst[:, 0 : P // 2], in_=w_raw[0][:].rearrange("p j (m t) -> p m j t", t=PACK))
+        w_src = w_raw[:].rearrange("p j (m t) -> p m j t", t=PACK)
+        nc.scalar.copy(out=w_dst[:, 0 : P // 2], in_=w_src[:, 0 : P // 2])
+        for q in range(4):
+            nc.vector.tensor_copy(out=xs[32 * q : 32 * q + 4, :].bitcast(I32), in_=xs_rows[32 * q : 32 * q + 4, :])
 
         xg_s = keep.tile([P, S], U8, name="xg_s", align_bytes=64)
         nc.vector.tensor_copy(out=xg_s[:], in_=xs[:].indirect(offs_t[:]))
 
-        nc.scalar.copy(out=w_dst[:, P // 2 : P], in_=w_raw[1][:].rearrange("p j (m t) -> p m j t", t=PACK))
+        nc.vector.tensor_copy(out=w_dst[:, P // 2 : P], in_=w_src[:, P // 2 : P])
         w_codes = keep.tile([P, N], U32, name="w_codes", align_bytes=64)
         w_sc = keep.tile([P, N], U8, name="w_sc", align_bytes=64)
         nc.vector.quantize_mx(out=w_codes[:].bitcast(FP8X4), scales=w_sc[:], in_=w_bf[:].rearrange("p t m j -> p (t m j)"))
 
-        xg_w = keep.tile([P, S], U32, name="xg_w", align_bytes=64)
+        xg_w = keep.tile([P, S], U32, name="xg_w", tag="w_bf_then_xg_w", align_bytes=64)
         for lo in (0, HALF):
             nc.vector.tensor_copy(out=xg_w[:, lo : lo + HALF], in_=xw[:].bitcast(U32).indirect(entries(offs_t, lo, lo + HALF)))
 
@@ -95,13 +99,13 @@ def tile_picked_cbn_none_po_kernel(tc, x_words, x_scales, w1, gamma, beta, offs,
         for t in range(1, PACK):
             nc.scalar.copy(out=y[:, t, :], in_=product(t, 0, S)[:])
 
-        nc.vector.tensor_copy(out=y[:, 0, :], in_=g_tab[0][:].indirect(cls_t[:]))
+        for lo in (0, HALF):
+            nc.vector.tensor_copy(out=y[:, 0, lo : lo + HALF], in_=g_tab[0][:].indirect(entries(cls_t, lo, lo + HALF)))
         for h in range(2):
             cols = slice(h * HALF, (h + 1) * HALF)
             nc.vector.tensor_tensor(out=yg[:, 0, cols], in0=acc0[h][:], in1=y[:, 0, cols], op=MULT)
         for t in range(PACK - 1):
-            if t + 1 < PACK - 1:
-                scale(t + 1, 0, S)
+            scale(t + 1, 0, S)
             shift(t, 0, S)
             nc.sync.dma_start(out=o_rows[:, t, :], in_=res[:, t, :])
 
@@ -120,13 +124,12 @@ def tile_picked_cbn_none_po_kernel(tc, x_words, x_scales, w1, gamma, beta, offs,
             nc.sync.dma_start(out=words_out[:, lo:hi], in_=o_codes[:, lo:hi])
 
         weave(nc.scalar.copy, 0, 0, S)
-        scale(3, 0, HALF)
-        scale(3, HALF, S)
         shift(3, 0, HALF)
         weave(nc.scalar.copy, 2, 0, HALF)
         shift(3, HALF, S)
         nc.sync.dma_start(out=o_rows[:, 3, :], in_=res[:, 3, :])
-        weave(nc.vector.tensor_copy, 2, HALF, S)
+        weave(nc.scalar.copy, 2, HALF, HALF + S // 4)
+        weave(nc.vector.tensor_copy, 2, HALF + S // 4, S)
         pack(0, HALF)
         pack(HALF, S)
         for q in range(4):

@@ -45,7 +45,7 @@ def tile_picked_cbn_none_po_kernel(tc, x_words, x_scales, w1, gamma, beta, offs,
 
         nc.vector.memset(xs[:].bitcast(I32), 0)
         for r in range(4):
-            nc.scalar.dma_start(out=xs_rows[r:P:32, :], in_=x_scales[0, r:16:4, :].bitcast(I32))
+            (nc.scalar if r < 2 else nc.sync).dma_start(out=xs_rows[r:P:32, :], in_=x_scales[0, r:16:4, :].bitcast(I32))
         nc.sync.dma_start(out=offs_t[:], in_=offs)
         nc.sync.dma_start(out=w_raw[:], in_=w_rows)
         nc.sync.dma_start(out=xw[:], in_=x_words[0].rearrange("p c r -> p (c r)").bitcast(I32))

@@ -17,7 +17,15 @@ ADD = mybir.AluOpType.add
 
 P = 128
 PACK = 4
+QUADRANT = 32
+SCALE_ROWS = 4
+QUADRANTS = P // QUADRANT
+LIST_ROWS = 16
 HALF = S // 2
+HALVES = (0, HALF)
+LAST = PACK - 1
+W_SPLIT = 48
+ROUND_SPLIT = HALF + HALF // 2
 
 
 def tile_picked_cbn_none_po_kernel(tc, x_words, x_scales, w1, gamma, beta, offs, cls, out_0, out_1, out_2):
@@ -26,112 +34,122 @@ def tile_picked_cbn_none_po_kernel(tc, x_words, x_scales, w1, gamma, beta, offs,
         keep = ctx.enter_context(tc.tile_pool(name="keep", bufs=1))
         psum = ctx.enter_context(tc.psum_pool(name="psum", bufs=1))
 
-        def entries(lst, lo, hi):
-            return lst[:, lo // 16 : hi // 16]
+        def entries(list_tile, lo, hi):
+            return list_tile[:, lo // LIST_ROWS : hi // LIST_ROWS]
 
-        offs_t = keep.tile([P, S // 16], U16, name="offs_t")
-        cls_t = keep.tile([P, S // 16], U16, name="cls_t")
-        xw = keep.tile([P, T], I32, name="xw", align_bytes=64)
-        xs = keep.tile([P, T], U8, name="xs", align_bytes=64)
-        xs_rows = keep.tile([P, T // 4], I32, name="xs_rows", align_bytes=64)
+        def scale_rows(tile, q):
+            return tile[QUADRANT * q : QUADRANT * q + SCALE_ROWS, :]
+
+        offs_t = keep.tile([P, S // LIST_ROWS], U16, name="offs_t")
+        cls_t = keep.tile([P, S // LIST_ROWS], U16, name="cls_t")
+        x_word_table = keep.tile([P, T], I32, name="x_word_table", align_bytes=64)
+        x_scale_table = keep.tile([P, T], U8, name="x_scale_table", align_bytes=64)
+        x_scale_landing = keep.tile([P, T // 4], I32, name="x_scale_landing", align_bytes=64)
         w_raw = keep.tile([P, PACK, N], F32, name="w_raw", align_bytes=64)
-        g_tab = [keep.tile([P, U], F32, name=f"g_tab{t}", align_bytes=64) for t in range(PACK)]
-        b_tab = [keep.tile([P, U], F32, name=f"b_tab{t}", align_bytes=64) for t in range(PACK)]
+        gamma_table = [keep.tile([P, U], F32, name=f"gamma_table{t}", align_bytes=64) for t in range(PACK)]
+        beta_table = [keep.tile([P, U], F32, name=f"beta_table{t}", align_bytes=64) for t in range(PACK)]
 
-        w_rows = w1.rearrange("(p j) c -> p j c", j=PACK)
-        g_rows = gamma.rearrange("(p t) u -> p t u", t=PACK)
-        b_rows = beta.rearrange("(p t) u -> p t u", t=PACK)
-        o_rows = out_0.rearrange("(p t) s -> p t s", t=PACK)
+        gamma_slots = gamma.rearrange("(p t) u -> p t u", t=PACK)
+        beta_slots = beta.rearrange("(p t) u -> p t u", t=PACK)
+        out_slots = out_0.rearrange("(p t) s -> p t s", t=PACK)
 
-        nc.vector.memset(xs[:].bitcast(I32), 0)
-        for r in range(4):
-            (nc.scalar if r < 2 else nc.sync).dma_start(out=xs_rows[r:P:32, :], in_=x_scales[0, r:16:4, :].bitcast(I32))
+        nc.vector.memset(x_scale_table[:].bitcast(I32), 0)
+
+        for r in range(SCALE_ROWS):
+            queue = nc.scalar if r < SCALE_ROWS // 2 else nc.sync
+            queue.dma_start(out=x_scale_landing[r:P:QUADRANT, :], in_=x_scales[0, r : QUADRANTS * SCALE_ROWS : SCALE_ROWS, :].bitcast(I32))
         nc.sync.dma_start(out=offs_t[:], in_=offs)
-        nc.sync.dma_start(out=w_raw[:], in_=w_rows)
-        nc.sync.dma_start(out=xw[:], in_=x_words[0].rearrange("p c r -> p (c r)").bitcast(I32))
+        nc.sync.dma_start(out=w_raw[:], in_=w1.rearrange("(p r) c -> p r c", r=PACK))
+        nc.sync.dma_start(out=x_word_table[:], in_=x_words[0].rearrange("p c r -> p (c r)").bitcast(I32))
         nc.sync.dma_start(out=cls_t[:], in_=cls)
-        for tab, rows, t in ((g_tab, g_rows, 0), (g_tab, g_rows, 1), (b_tab, b_rows, 0), (g_tab, g_rows, 2), (b_tab, b_rows, 1), (g_tab, g_rows, 3), (b_tab, b_rows, 2), (b_tab, b_rows, 3)):
-            nc.sync.dma_start(out=tab[t][:], in_=rows[:, t, :])
+        nc.sync.dma_start(out=gamma_table[0][:], in_=gamma_slots[:, 0, :])
+        for t in range(PACK):
+            if t < LAST:
+                nc.sync.dma_start(out=gamma_table[t + 1][:], in_=gamma_slots[:, t + 1, :])
+            nc.sync.dma_start(out=beta_table[t][:], in_=beta_slots[:, t, :])
 
-        w_bf = keep.tile([P, PACK, P, PACK], BF16, name="w_bf", tag="w_bf_then_xg_w", align_bytes=64)
-        w_dst = w_bf[:].rearrange("p t m j -> p m j t")
-        w_src = w_raw[:].rearrange("p j (m t) -> p m j t", t=PACK)
-        nc.scalar.copy(out=w_dst[:, 0 : P // 2], in_=w_src[:, 0 : P // 2])
-        for q in range(4):
-            nc.vector.tensor_copy(out=xs[32 * q : 32 * q + 4, :].bitcast(I32), in_=xs_rows[32 * q : 32 * q + 4, :])
+        w_bf = keep.tile([P, PACK, P, PACK], BF16, name="w_bf", tag="w_bf_then_picked_words", align_bytes=64)
+        w_dst = w_bf[:].rearrange("p t m r -> p m r t")
+        w_src = w_raw[:].rearrange("p r (m t) -> p m r t", t=PACK)
+        nc.scalar.copy(out=w_dst[:, 0:W_SPLIT], in_=w_src[:, 0:W_SPLIT])
 
-        xg_s = keep.tile([P, S], U8, name="xg_s", align_bytes=64)
-        nc.vector.tensor_copy(out=xg_s[:], in_=xs[:].indirect(offs_t[:]))
+        for q in range(QUADRANTS):
+            nc.vector.tensor_copy(out=scale_rows(x_scale_table, q).bitcast(I32), in_=scale_rows(x_scale_landing, q))
+        picked_scales = keep.tile([P, S], U8, name="picked_scales", align_bytes=64)
+        nc.vector.tensor_copy(out=picked_scales[:], in_=x_scale_table[:].indirect(offs_t[:]))
 
-        nc.vector.tensor_copy(out=w_dst[:, P // 2 : P], in_=w_src[:, P // 2 : P])
+        nc.vector.tensor_copy(out=w_dst[:, W_SPLIT:P], in_=w_src[:, W_SPLIT:P])
         w_codes = keep.tile([P, N], U32, name="w_codes", align_bytes=64)
-        w_sc = keep.tile([P, N], U8, name="w_sc", align_bytes=64)
-        nc.vector.quantize_mx(out=w_codes[:].bitcast(FP8X4), scales=w_sc[:], in_=w_bf[:].rearrange("p t m j -> p (t m j)"))
+        w_scales = keep.tile([P, N], U8, name="w_scales", align_bytes=64)
+        nc.vector.quantize_mx(out=w_codes[:].bitcast(FP8X4), scales=w_scales[:], in_=w_bf[:].rearrange("p t m r -> p (t m r)"))
 
-        xg_w = keep.tile([P, S], U32, name="xg_w", tag="w_bf_then_xg_w", align_bytes=64)
-        for lo in (0, HALF):
-            nc.vector.tensor_copy(out=xg_w[:, lo : lo + HALF], in_=xw[:].bitcast(U32).indirect(entries(offs_t, lo, lo + HALF)))
+        picked_words = keep.tile([P, S], U32, name="picked_words", tag="w_bf_then_picked_words", align_bytes=64)
+        for lo in HALVES:
+            nc.vector.tensor_copy(out=picked_words[:, lo : lo + HALF], in_=x_word_table[:].bitcast(U32).indirect(entries(offs_t, lo, lo + HALF)))
 
-        y = keep.tile([P, PACK, S], F32, name="y", align_bytes=64)
-        yg = keep.tile([P, PACK, S], F32, name="yg", align_bytes=64)
-        res = keep.tile([P, PACK, S], F32, name="res", align_bytes=64)
+        picked_gamma0 = keep.tile([P, S], F32, name="picked_gamma0", align_bytes=64)
+        y = keep.tile([P, LAST, S], F32, name="y", align_bytes=64)
+        scaled = keep.tile([P, PACK, S], F32, name="scaled", align_bytes=64)
+        result = keep.tile([P, PACK, S], F32, name="result", align_bytes=64)
 
         def product(t, lo, hi):
             acc = psum.tile([P, hi - lo], F32, name=f"acc{t}_{lo}")
             nc.tensor.matmul_mx(
                 out=acc[:],
                 lhsT=w_codes[:, t * P : (t + 1) * P].bitcast(FP8X4),
-                lhsT_scale=w_sc[:, t * P : (t + 1) * P],
-                rhs=xg_w[:, lo:hi].bitcast(FP8X4),
-                rhs_scale=xg_s[:, lo:hi],
+                lhsT_scale=w_scales[:, t * P : (t + 1) * P],
+                rhs=picked_words[:, lo:hi].bitcast(FP8X4),
+                rhs_scale=picked_scales[:, lo:hi],
                 start=True,
                 stop=True,
             )
             return acc
 
-        def scale(t, lo, hi):
-            nc.vector.tensor_tensor(out=yg[:, t, lo:hi], in0=g_tab[t][:].indirect(entries(cls_t, lo, hi)), in1=y[:, t, lo:hi], op=MULT)
+        def add_beta(t, lo, hi):
+            nc.vector.tensor_tensor(out=result[:, t, lo:hi], in0=beta_table[t][:].indirect(entries(cls_t, lo, hi)), in1=scaled[:, t, lo:hi], op=ADD)
 
-        def shift(t, lo, hi):
-            nc.vector.tensor_tensor(out=res[:, t, lo:hi], in0=b_tab[t][:].indirect(entries(cls_t, lo, hi)), in1=yg[:, t, lo:hi], op=ADD)
+        acc0 = []
+        for lo in HALVES:
+            acc0.append(product(0, lo, lo + HALF))
+            nc.scalar.copy(out=y[:, 0, lo : lo + HALF], in_=product(1, lo, lo + HALF)[:])
+        for t in range(2, PACK):
+            nc.scalar.copy(out=y[:, t - 1, :], in_=product(t, 0, S)[:])
 
-        acc0 = [product(0, lo, lo + HALF) for lo in (0, HALF)]
-        for t in range(1, PACK):
-            nc.scalar.copy(out=y[:, t, :], in_=product(t, 0, S)[:])
+        for lo in HALVES:
+            nc.vector.tensor_copy(out=picked_gamma0[:, lo : lo + HALF], in_=gamma_table[0][:].indirect(entries(cls_t, lo, lo + HALF)))
+        for h, lo in enumerate(HALVES):
+            nc.vector.tensor_tensor(out=scaled[:, 0, lo : lo + HALF], in0=acc0[h][:], in1=picked_gamma0[:, lo : lo + HALF], op=MULT)
 
-        for lo in (0, HALF):
-            nc.vector.tensor_copy(out=y[:, 0, lo : lo + HALF], in_=g_tab[0][:].indirect(entries(cls_t, lo, lo + HALF)))
-        for h in range(2):
-            cols = slice(h * HALF, (h + 1) * HALF)
-            nc.vector.tensor_tensor(out=yg[:, 0, cols], in0=acc0[h][:], in1=y[:, 0, cols], op=MULT)
-        for t in range(PACK - 1):
-            scale(t + 1, 0, S)
-            shift(t, 0, S)
-            nc.sync.dma_start(out=o_rows[:, t, :], in_=res[:, t, :])
+        for t in range(LAST):
+            nc.vector.tensor_tensor(out=scaled[:, t + 1, :], in0=gamma_table[t + 1][:].indirect(cls_t[:]), in1=y[:, t, :], op=MULT)
+            add_beta(t, 0, S)
+            nc.sync.dma_start(out=out_slots[:, t, :], in_=result[:, t, :])
 
-        o_bf = keep.tile([P, S, PACK], BF16, name="o_bf", align_bytes=64)
-        o_codes = keep.tile([P, S], I32, name="o_codes", align_bytes=64)
-        o_sc = keep.tile([P, S], U8, name="o_sc", align_bytes=64)
-        words_out = out_1[0].rearrange("p c r -> p (c r)").bitcast(I32)
+        rounded = [keep.tile([P, HALF, PACK], BF16, name=f"rounded{h}", align_bytes=64) for h in range(len(HALVES))]
+        out_codes = keep.tile([P, S], I32, name="out_codes", align_bytes=64)
+        out_scales = keep.tile([P, S], U8, name="out_scales", align_bytes=64)
+        out_words = out_1[0].rearrange("p c r -> p (c r)").bitcast(I32)
 
-        def weave(engine_copy, t0, lo, hi):
-            engine_copy(out=o_bf[:, lo:hi, t0 : t0 + 2], in_=res[:, t0 : t0 + 2, lo:hi].rearrange("p t c -> p c t"))
+        def round_pair(copy, t, lo, hi):
+            h = lo // HALF
+            copy(out=rounded[h][:, lo - HALVES[h] : hi - HALVES[h], t : t + 2], in_=result[:, t : t + 2, lo:hi].rearrange("p t c -> p c t"))
 
-        def pack(lo, hi):
-            nc.vector.quantize_mx(
-                out=o_codes[:, lo:hi].bitcast(FP8X4), scales=o_sc[:, lo:hi], in_=o_bf[:].rearrange("p c t -> p (c t)")[:, PACK * lo : PACK * hi]
-            )
-            nc.sync.dma_start(out=words_out[:, lo:hi], in_=o_codes[:, lo:hi])
+        def quantise_half(h):
+            cols = slice(HALVES[h], HALVES[h] + HALF)
+            nc.vector.quantize_mx(out=out_codes[:, cols].bitcast(FP8X4), scales=out_scales[:, cols], in_=rounded[h][:].rearrange("p c t -> p (c t)"))
+            nc.sync.dma_start(out=out_words[:, cols], in_=out_codes[:, cols])
 
-        weave(nc.scalar.copy, 0, 0, S)
-        shift(3, 0, HALF)
-        weave(nc.scalar.copy, 2, 0, HALF)
-        shift(3, HALF, S)
-        nc.sync.dma_start(out=o_rows[:, 3, :], in_=res[:, 3, :])
-        weave(nc.scalar.copy, 2, HALF, HALF + S // 4)
-        weave(nc.vector.tensor_copy, 2, HALF + S // 4, S)
-        pack(0, HALF)
-        pack(HALF, S)
-        for q in range(4):
-            eng = nc.scalar if q % 2 == 0 else nc.sync
-            eng.dma_start(out=out_2[0, 4 * q : 4 * q + 4, :].bitcast(I32), in_=o_sc[32 * q : 32 * q + 4, :].bitcast(I32))
+        for lo in HALVES:
+            round_pair(nc.scalar.copy, 0, lo, lo + HALF)
+        add_beta(LAST, 0, HALF)
+        round_pair(nc.scalar.copy, 2, 0, HALF)
+        add_beta(LAST, HALF, S)
+        nc.sync.dma_start(out=out_slots[:, LAST, :], in_=result[:, LAST, :])
+        round_pair(nc.scalar.copy, 2, HALF, ROUND_SPLIT)
+        round_pair(nc.vector.tensor_copy, 2, ROUND_SPLIT, S)
+        for h in range(len(HALVES)):
+            quantise_half(h)
+
+        for q in range(QUADRANTS):
+            queue = nc.scalar if q % 2 == 0 else nc.sync
+            queue.dma_start(out=out_2[0, SCALE_ROWS * q : SCALE_ROWS * (q + 1), :].bitcast(I32), in_=scale_rows(out_scales, q).bitcast(I32))

@@ -25,7 +25,7 @@ HALF = S // 2
 HALVES = (0, HALF)
 LAST = PACK - 1
 W_SPLIT = 48
-ROUND_SPLIT = HALF + HALF // 2
+ROUND_SPLITS = (HALF // 2, HALF + HALF // 4)
 
 
 def tile_picked_cbn_none_po_kernel(tc, x_words, x_scales, w1, gamma, beta, offs, cls, out_0, out_1, out_2):
@@ -87,7 +87,8 @@ def tile_picked_cbn_none_po_kernel(tc, x_words, x_scales, w1, gamma, beta, offs,
         for lo in HALVES:
             nc.vector.tensor_copy(out=picked_words[:, lo : lo + HALF], in_=x_word_table[:].bitcast(U32).indirect(entries(offs_t, lo, lo + HALF)))
 
-        picked_gamma0 = keep.tile([P, S], F32, name="picked_gamma0", align_bytes=64)
+        picked_gamma0 = keep.tile([P, HALF], F32, name="picked_gamma0", align_bytes=64)
+        y0 = keep.tile([P, HALF], F32, name="y0", align_bytes=64)
         y = keep.tile([P, LAST, S], F32, name="y", align_bytes=64)
         scaled = keep.tile([P, PACK, S], F32, name="scaled", align_bytes=64)
         result = keep.tile([P, PACK, S], F32, name="result", align_bytes=64)
@@ -108,17 +109,17 @@ def tile_picked_cbn_none_po_kernel(tc, x_words, x_scales, w1, gamma, beta, offs,
         def add_beta(t, lo, hi):
             nc.vector.tensor_tensor(out=result[:, t, lo:hi], in0=beta_table[t][:].indirect(entries(cls_t, lo, hi)), in1=scaled[:, t, lo:hi], op=ADD)
 
-        acc0 = []
-        for lo in HALVES:
-            acc0.append(product(0, lo, lo + HALF))
-            nc.scalar.copy(out=y[:, 0, lo : lo + HALF], in_=product(1, lo, lo + HALF)[:])
+        for lo in (0, HALF // 2):
+            nc.scalar.copy(out=y0[:, lo : lo + HALF // 2], in_=product(0, lo, lo + HALF // 2)[:])
+        nc.scalar.copy(out=y[:, 0, 0:HALF], in_=product(1, 0, HALF)[:])
+        nc.scalar.copy(out=y[:, 0, HALF:S], in_=product(1, HALF, S)[:])
+        acc0 = product(0, HALF, S)
         for t in range(2, PACK):
             nc.scalar.copy(out=y[:, t - 1, :], in_=product(t, 0, S)[:])
 
-        for lo in HALVES:
-            nc.vector.tensor_copy(out=picked_gamma0[:, lo : lo + HALF], in_=gamma_table[0][:].indirect(entries(cls_t, lo, lo + HALF)))
-        for h, lo in enumerate(HALVES):
-            nc.vector.tensor_tensor(out=scaled[:, 0, lo : lo + HALF], in0=acc0[h][:], in1=picked_gamma0[:, lo : lo + HALF], op=MULT)
+        nc.vector.tensor_copy(out=picked_gamma0[:], in_=gamma_table[0][:].indirect(entries(cls_t, HALF, S)))
+        nc.vector.tensor_tensor(out=scaled[:, 0, 0:HALF], in0=gamma_table[0][:].indirect(entries(cls_t, 0, HALF)), in1=y0[:], op=MULT)
+        nc.vector.tensor_tensor(out=scaled[:, 0, HALF:S], in0=acc0[:], in1=picked_gamma0[:], op=MULT)
 
         for t in range(LAST):
             nc.vector.tensor_tensor(out=scaled[:, t + 1, :], in0=gamma_table[t + 1][:].indirect(cls_t[:]), in1=y[:, t, :], op=MULT)
@@ -142,11 +143,11 @@ def tile_picked_cbn_none_po_kernel(tc, x_words, x_scales, w1, gamma, beta, offs,
         for lo in HALVES:
             round_pair(nc.scalar.copy, 0, lo, lo + HALF)
         add_beta(LAST, 0, HALF)
-        round_pair(nc.scalar.copy, 2, 0, HALF)
         add_beta(LAST, HALF, S)
         nc.sync.dma_start(out=out_slots[:, LAST, :], in_=result[:, LAST, :])
-        round_pair(nc.scalar.copy, 2, HALF, ROUND_SPLIT)
-        round_pair(nc.vector.tensor_copy, 2, ROUND_SPLIT, S)
+        for lo, split in zip(HALVES, ROUND_SPLITS):
+            round_pair(nc.scalar.copy, 2, lo, split)
+            round_pair(nc.vector.tensor_copy, 2, split, lo + HALF)
         for h in range(len(HALVES)):
             quantise_half(h)
 

@@ -1,6 +1,7 @@
 from contextlib import ExitStack
 
 import concourse.mybir as mybir
+from concourse.masks import make_identity
 
 K, T, S, N, U = 512, 2048, 512, 512, 1024
 FLOPS = 2 * K * N * S
@@ -24,6 +25,8 @@ LIST_ROWS = 16
 HALF = S // 2
 HALVES = (0, HALF)
 LAST = PACK - 1
+EARLY, LATE = (0, 1), (2, 3)
+BLOCKS = HALF // P
 W_SPLIT = 48
 ROUND_SPLITS = (HALF // 2, HALF + HALF // 4)
 
@@ -62,11 +65,15 @@ def tile_picked_cbn_none_po_kernel(tc, x_words, x_scales, w1, gamma, beta, offs,
         nc.sync.dma_start(out=w_raw[:], in_=w1.rearrange("(p r) c -> p r c", r=PACK))
         nc.sync.dma_start(out=x_word_table[:], in_=x_words[0].rearrange("p c r -> p (c r)").bitcast(I32))
         nc.sync.dma_start(out=cls_t[:], in_=cls)
-        nc.sync.dma_start(out=gamma_table[0][:], in_=gamma_slots[:, 0, :])
-        for t in range(PACK):
-            if t < LAST:
-                nc.sync.dma_start(out=gamma_table[t + 1][:], in_=gamma_slots[:, t + 1, :])
+        for t in EARLY:
             nc.sync.dma_start(out=beta_table[t][:], in_=beta_slots[:, t, :])
+        for t in range(PACK):
+            nc.sync.dma_start(out=gamma_table[t][:], in_=gamma_slots[:, t, :])
+        for t in LATE:
+            nc.sync.dma_start(out=beta_table[t][:], in_=beta_slots[:, t, :])
+
+        identity = keep.tile([P, P], F32, name="identity")
+        make_identity(nc, identity[:])
 
         w_bf = keep.tile([P, PACK, P, PACK], BF16, name="w_bf", tag="w_bf_then_picked_words", align_bytes=64)
         w_dst = w_bf[:].rearrange("p t m r -> p m r t")
@@ -84,47 +91,54 @@ def tile_picked_cbn_none_po_kernel(tc, x_words, x_scales, w1, gamma, beta, offs,
         nc.vector.quantize_mx(out=w_codes[:].bitcast(FP8X4), scales=w_scales[:], in_=w_bf[:].rearrange("p t m r -> p (t m r)"))
 
         picked_words = keep.tile([P, S], U32, name="picked_words", tag="w_bf_then_picked_words", align_bytes=64)
-        for lo in HALVES:
-            nc.vector.tensor_copy(out=picked_words[:, lo : lo + HALF], in_=x_word_table[:].bitcast(U32).indirect(entries(offs_t, lo, lo + HALF)))
+        nc.vector.tensor_copy(out=picked_words[:], in_=x_word_table[:].bitcast(U32).indirect(offs_t[:]))
 
-        picked_gamma0 = keep.tile([P, HALF], F32, name="picked_gamma0", align_bytes=64)
-        y0 = keep.tile([P, HALF], F32, name="y0", align_bytes=64)
-        y = keep.tile([P, LAST, S], F32, name="y", align_bytes=64)
+        picked_beta = keep.tile([P, len(EARLY), S], F32, name="picked_beta", align_bytes=64)
+        y = keep.tile([P, PACK, S], F32, name="y", align_bytes=64)
         scaled = keep.tile([P, PACK, S], F32, name="scaled", align_bytes=64)
+        turned = keep.tile([P, len(EARLY), S], F32, name="turned", align_bytes=64)
         result = keep.tile([P, PACK, S], F32, name="result", align_bytes=64)
 
-        def product(t, lo, hi):
-            acc = psum.tile([P, hi - lo], F32, name=f"acc{t}_{lo}")
+        for t in range(PACK):
+            acc = psum.tile([P, S], F32, name=f"acc{t}", tag=f"bank{t}")
             nc.tensor.matmul_mx(
                 out=acc[:],
                 lhsT=w_codes[:, t * P : (t + 1) * P].bitcast(FP8X4),
                 lhsT_scale=w_scales[:, t * P : (t + 1) * P],
-                rhs=picked_words[:, lo:hi].bitcast(FP8X4),
-                rhs_scale=picked_scales[:, lo:hi],
+                rhs=picked_words[:].bitcast(FP8X4),
+                rhs_scale=picked_scales[:],
                 start=True,
                 stop=True,
             )
-            return acc
+            nc.scalar.copy(out=y[:, t, :], in_=acc[:])
+
+        def turn(bank, source, lo, start, stop):
+            for i in range(BLOCKS):
+                cols = slice(lo + i * P, lo + (i + 1) * P)
+                nc.tensor.matmul(out=bank[:, i * P : (i + 1) * P], lhsT=source[:, cols], rhs=identity[:], is_transpose=True, start=start and i == 0, stop=stop and i == BLOCKS - 1)
 
         def add_beta(t, lo, hi):
             nc.vector.tensor_tensor(out=result[:, t, lo:hi], in0=beta_table[t][:].indirect(entries(cls_t, lo, hi)), in1=scaled[:, t, lo:hi], op=ADD)
 
-        for lo in (0, HALF // 2):
-            nc.scalar.copy(out=y0[:, lo : lo + HALF // 2], in_=product(0, lo, lo + HALF // 2)[:])
-        nc.scalar.copy(out=y[:, 0, 0:HALF], in_=product(1, 0, HALF)[:])
-        nc.scalar.copy(out=y[:, 0, HALF:S], in_=product(1, HALF, S)[:])
-        acc0 = product(0, HALF, S)
-        for t in range(2, PACK):
-            nc.scalar.copy(out=y[:, t - 1, :], in_=product(t, 0, S)[:])
-
-        nc.vector.tensor_copy(out=picked_gamma0[:], in_=gamma_table[0][:].indirect(entries(cls_t, HALF, S)))
-        nc.vector.tensor_tensor(out=scaled[:, 0, 0:HALF], in0=gamma_table[0][:].indirect(entries(cls_t, 0, HALF)), in1=y0[:], op=MULT)
-        nc.vector.tensor_tensor(out=scaled[:, 0, HALF:S], in0=acc0[:], in1=picked_gamma0[:], op=MULT)
-
-        for t in range(LAST):
-            nc.vector.tensor_tensor(out=scaled[:, t + 1, :], in0=gamma_table[t + 1][:].indirect(cls_t[:]), in1=y[:, t, :], op=MULT)
-            add_beta(t, 0, S)
-            nc.sync.dma_start(out=out_slots[:, t, :], in_=result[:, t, :])
+        sums = {}
+        for t in EARLY:
+            nc.vector.tensor_copy(out=picked_beta[:, t, :], in_=beta_table[t][:].indirect(cls_t[:]))
+            for lo in HALVES:
+                sums[t, lo] = psum.tile([P, HALF], F32, name=f"sum{t}_{lo}")
+                turn(sums[t, lo], picked_beta[:, t, :], lo, True, False)
+        for t in range(PACK):
+            nc.vector.tensor_tensor(out=scaled[:, t, :], in0=gamma_table[t][:].indirect(cls_t[:]), in1=y[:, t, :], op=MULT)
+        for t in EARLY:
+            for lo in HALVES:
+                turn(sums[t, lo], scaled[:, t, :], lo, False, True)
+                nc.scalar.copy(out=turned[:, t, lo : lo + HALF], in_=sums[t, lo][:])
+            for h, lo in enumerate(HALVES):
+                back = psum.tile([P, HALF], F32, name=f"back{t}_{lo}", tag=f"bank{2 * t + h}")
+                turn(back, turned[:, t, :], lo, True, True)
+                nc.scalar.copy(out=result[:, t, lo : lo + HALF], in_=back[:])
+        nc.sync.dma_start(out=out_slots[:, 0:2, :], in_=result[:, 0:2, :])
+        add_beta(2, 0, S)
+        nc.sync.dma_start(out=out_slots[:, 2, :], in_=result[:, 2, :])
 
         rounded = [keep.tile([P, HALF, PACK], BF16, name=f"rounded{h}", align_bytes=64) for h in range(len(HALVES))]
         out_codes = keep.tile([P, S], I32, name="out_codes", align_bytes=64)

@@ -27,6 +27,9 @@ HALVES = (0, HALF)
 LAST = PACK - 1
 EARLY, LATE = (0, 1), (2, 3)
 BLOCKS = HALF // P
+TABLE_BYTES = 4 * U
+RING = 4
+LANDING = 16
 W_SPLIT = 48
 ROUND_SPLITS = (HALF // 2, HALF + HALF // 4)
 
@@ -35,6 +38,7 @@ def tile_picked_cbn_none_po_kernel(tc, x_words, x_scales, w1, gamma, beta, offs,
     nc = tc.nc
     with ExitStack() as ctx:
         keep = ctx.enter_context(tc.tile_pool(name="keep", bufs=1))
+        ring = ctx.enter_context(tc.tile_pool(name="ring", bufs=1))
         psum = ctx.enter_context(tc.psum_pool(name="psum", bufs=1))
 
         def entries(list_tile, lo, hi):
@@ -46,31 +50,28 @@ def tile_picked_cbn_none_po_kernel(tc, x_words, x_scales, w1, gamma, beta, offs,
         offs_t = keep.tile([P, S // LIST_ROWS], U16, name="offs_t")
         cls_t = keep.tile([P, S // LIST_ROWS], U16, name="cls_t")
         x_word_table = keep.tile([P, T], I32, name="x_word_table", align_bytes=64)
-        x_scale_table = keep.tile([P, T], U8, name="x_scale_table", align_bytes=64)
-        x_scale_landing = keep.tile([P, T // 4], I32, name="x_scale_landing", align_bytes=64)
-        w_raw = keep.tile([P, PACK, N], F32, name="w_raw", align_bytes=64)
-        gamma_table = [keep.tile([P, U], F32, name=f"gamma_table{t}", align_bytes=64) for t in range(PACK)]
-        beta_table = [keep.tile([P, U], F32, name=f"beta_table{t}", align_bytes=64) for t in range(PACK)]
+        x_scale_table = ring.tile([P, T], U8, name="x_scale_table", offset=0)
+        w_raw = ring.tile([P, PACK, N], F32, name="w_raw", offset=TABLE_BYTES + TABLE_BYTES // 2)
+        gamma_table, beta_table = {}, {}
 
         gamma_slots = gamma.rearrange("(p t) u -> p t u", t=PACK)
         beta_slots = beta.rearrange("(p t) u -> p t u", t=PACK)
         out_slots = out_0.rearrange("(p t) s -> p t s", t=PACK)
 
-        nc.vector.memset(x_scale_table[:].bitcast(I32), 0)
-
-        for r in range(SCALE_ROWS):
-            queue = nc.scalar if r < SCALE_ROWS // 2 else nc.sync
-            queue.dma_start(out=x_scale_landing[r:P:QUADRANT, :], in_=x_scales[0, r : QUADRANTS * SCALE_ROWS : SCALE_ROWS, :].bitcast(I32))
+        nc.scalar.dma_start(out=x_scale_table[LANDING:QUADRANT, :].bitcast(I32), in_=x_scales[0].bitcast(I32))
+        for lo, hi in ((0, LANDING), (QUADRANT, 2 * QUADRANT), (2 * QUADRANT, P)):
+            nc.vector.memset(x_scale_table[lo:hi, :].bitcast(I32), 0)
+        picked_scales = keep.tile([P, S], U8, name="picked_scales", align_bytes=64)
+        nc.vector.memset(picked_scales[:].bitcast(I32), 0)
         nc.sync.dma_start(out=offs_t[:], in_=offs)
+        nc.sync.dma_start(out=cls_t[:], in_=cls)
         nc.sync.dma_start(out=w_raw[:], in_=w1.rearrange("(p r) c -> p r c", r=PACK))
         nc.sync.dma_start(out=x_word_table[:], in_=x_words[0].rearrange("p c r -> p (c r)").bitcast(I32))
-        nc.sync.dma_start(out=cls_t[:], in_=cls)
-        for t in EARLY:
-            nc.sync.dma_start(out=beta_table[t][:], in_=beta_slots[:, t, :])
-        for t in range(PACK):
-            nc.sync.dma_start(out=gamma_table[t][:], in_=gamma_slots[:, t, :])
-        for t in LATE:
-            nc.sync.dma_start(out=beta_table[t][:], in_=beta_slots[:, t, :])
+
+        def load_table(tables, slots, name, t):
+            place = (len(gamma_table) + len(beta_table)) % RING
+            tables[t] = ring.tile([P, U], F32, name=f"{name}{t}", offset=place * TABLE_BYTES)
+            nc.sync.dma_start(out=tables[t][:], in_=slots[:, t, :])
 
         identity = keep.tile([P, P], F32, name="identity")
         make_identity(nc, identity[:])
@@ -80,12 +81,16 @@ def tile_picked_cbn_none_po_kernel(tc, x_words, x_scales, w1, gamma, beta, offs,
         w_src = w_raw[:].rearrange("p r (m t) -> p m r t", t=PACK)
         nc.scalar.copy(out=w_dst[:, 0:W_SPLIT], in_=w_src[:, 0:W_SPLIT])
 
-        for q in range(QUADRANTS):
-            nc.vector.tensor_copy(out=scale_rows(x_scale_table, q).bitcast(I32), in_=scale_rows(x_scale_landing, q))
-        picked_scales = keep.tile([P, S], U8, name="picked_scales", align_bytes=64)
-        nc.vector.tensor_copy(out=picked_scales[:], in_=x_scale_table[:].indirect(offs_t[:]))
+        picked_landing = keep.tile([P, S], U8, name="picked_landing", align_bytes=64)
+        nc.vector.tensor_copy(out=picked_landing[:], in_=x_scale_table[:].indirect(offs_t[:]))
+        for r in range(SCALE_ROWS):
+            nc.sync.dma_start(out=picked_scales[r:P:QUADRANT, :].bitcast(I32), in_=picked_landing[LANDING + r : QUADRANT : SCALE_ROWS, :].bitcast(I32))
+        load_table(beta_table, beta_slots, "beta_table", 0)
 
         nc.vector.tensor_copy(out=w_dst[:, W_SPLIT:P], in_=w_src[:, W_SPLIT:P])
+        load_table(beta_table, beta_slots, "beta_table", 1)
+        for t in EARLY:
+            load_table(gamma_table, gamma_slots, "gamma_table", t)
         w_codes = keep.tile([P, N], U32, name="w_codes", align_bytes=64)
         w_scales = keep.tile([P, N], U8, name="w_scales", align_bytes=64)
         nc.vector.quantize_mx(out=w_codes[:].bitcast(FP8X4), scales=w_scales[:], in_=w_bf[:].rearrange("p t m r -> p (t m r)"))
@@ -123,11 +128,14 @@ def tile_picked_cbn_none_po_kernel(tc, x_words, x_scales, w1, gamma, beta, offs,
         sums = {}
         for t in EARLY:
             nc.vector.tensor_copy(out=picked_beta[:, t, :], in_=beta_table[t][:].indirect(cls_t[:]))
+            load_table(gamma_table, gamma_slots, "gamma_table", LATE[t])
             for lo in HALVES:
                 sums[t, lo] = psum.tile([P, HALF], F32, name=f"sum{t}_{lo}")
                 turn(sums[t, lo], picked_beta[:, t, :], lo, True, False)
         for t in range(PACK):
             nc.vector.tensor_tensor(out=scaled[:, t, :], in0=gamma_table[t][:].indirect(cls_t[:]), in1=y[:, t, :], op=MULT)
+            if t in EARLY:
+                load_table(beta_table, beta_slots, "beta_table", LATE[t])
         for t in EARLY:
             for lo in HALVES:
                 turn(sums[t, lo], scaled[:, t, :], lo, False, True)

@@ -28,7 +28,7 @@ LAST = PACK - 1
 EARLY, LATE = (0, 1), (2, 3)
 BLOCKS = HALF // P
 TABLE_BYTES = 4 * U
-RING = 4
+RING = 7
 LANDING = 16
 W_SPLIT = 48
 ROUND_SPLITS = (HALF // 2, HALF + HALF // 4)
@@ -49,7 +49,7 @@ def tile_picked_cbn_none_po_kernel(tc, x_words, x_scales, w1, gamma, beta, offs,
 
         offs_t = keep.tile([P, S // LIST_ROWS], U16, name="offs_t")
         cls_t = keep.tile([P, S // LIST_ROWS], U16, name="cls_t")
-        x_word_table = keep.tile([P, T], I32, name="x_word_table", align_bytes=64)
+        x_word_table = ring.tile([P, T], I32, name="x_word_table", offset=4 * TABLE_BYTES + TABLE_BYTES // 2)
         x_scale_table = ring.tile([P, T], U8, name="x_scale_table", offset=0)
         w_raw = ring.tile([P, PACK, N], F32, name="w_raw", offset=TABLE_BYTES + TABLE_BYTES // 2)
         gamma_table, beta_table = {}, {}
@@ -97,6 +97,9 @@ def tile_picked_cbn_none_po_kernel(tc, x_words, x_scales, w1, gamma, beta, offs,
 
         picked_words = keep.tile([P, S], U32, name="picked_words", tag="w_bf_then_picked_words", align_bytes=64)
         nc.vector.tensor_copy(out=picked_words[:], in_=x_word_table[:].bitcast(U32).indirect(offs_t[:]))
+        for t in LATE:
+            load_table(gamma_table, gamma_slots, "gamma_table", t)
+        load_table(beta_table, beta_slots, "beta_table", LATE[0])
 
         picked_beta = keep.tile([P, len(EARLY), S], F32, name="picked_beta", align_bytes=64)
         y = keep.tile([P, PACK, S], F32, name="y", align_bytes=64)
@@ -128,14 +131,13 @@ def tile_picked_cbn_none_po_kernel(tc, x_words, x_scales, w1, gamma, beta, offs,
         sums = {}
         for t in EARLY:
             nc.vector.tensor_copy(out=picked_beta[:, t, :], in_=beta_table[t][:].indirect(cls_t[:]))
-            load_table(gamma_table, gamma_slots, "gamma_table", LATE[t])
+            if t == 0:
+                load_table(beta_table, beta_slots, "beta_table", LAST)
             for lo in HALVES:
                 sums[t, lo] = psum.tile([P, HALF], F32, name=f"sum{t}_{lo}")
                 turn(sums[t, lo], picked_beta[:, t, :], lo, True, False)
         for t in range(PACK):
             nc.vector.tensor_tensor(out=scaled[:, t, :], in0=gamma_table[t][:].indirect(cls_t[:]), in1=y[:, t, :], op=MULT)
-            if t in EARLY:
-                load_table(beta_table, beta_slots, "beta_table", LATE[t])
         for t in EARLY:
             for lo in HALVES:
                 turn(sums[t, lo], scaled[:, t, :], lo, False, True)

@@ -28,7 +28,7 @@ LAST = PACK - 1
 EARLY, LATE = (0, 1), (2, 3)
 BLOCKS = HALF // P
 TABLE_BYTES = 4 * U
-RING = 7
+RING = 8
 LANDING = 16
 W_SPLIT = 48
 ROUND_SPLITS = (HALF // 2, HALF + HALF // 4)
@@ -64,14 +64,16 @@ def tile_picked_cbn_none_po_kernel(tc, x_words, x_scales, w1, gamma, beta, offs,
         picked_scales = keep.tile([P, S], U8, name="picked_scales", align_bytes=64)
         nc.vector.memset(picked_scales[:].bitcast(I32), 0)
         nc.sync.dma_start(out=offs_t[:], in_=offs)
-        nc.sync.dma_start(out=cls_t[:], in_=cls)
         nc.sync.dma_start(out=w_raw[:], in_=w1.rearrange("(p r) c -> p r c", r=PACK))
         nc.sync.dma_start(out=x_word_table[:], in_=x_words[0].rearrange("p c r -> p (c r)").bitcast(I32))
+        nc.sync.dma_start(out=cls_t[:], in_=cls)
 
         def load_table(tables, slots, name, t):
-            place = (len(gamma_table) + len(beta_table)) % RING
+            place = (len(gamma_table) + len(beta_table) - 1) % RING
             tables[t] = ring.tile([P, U], F32, name=f"{name}{t}", offset=place * TABLE_BYTES)
             nc.sync.dma_start(out=tables[t][:], in_=slots[:, t, :])
+
+        load_table(beta_table, beta_slots, "beta_table", 0)
 
         identity = keep.tile([P, P], F32, name="identity")
         make_identity(nc, identity[:])
@@ -85,11 +87,10 @@ def tile_picked_cbn_none_po_kernel(tc, x_words, x_scales, w1, gamma, beta, offs,
         nc.vector.tensor_copy(out=picked_landing[:], in_=x_scale_table[:].indirect(offs_t[:]))
         for r in range(SCALE_ROWS):
             nc.sync.dma_start(out=picked_scales[r:P:QUADRANT, :].bitcast(I32), in_=picked_landing[LANDING + r : QUADRANT : SCALE_ROWS, :].bitcast(I32))
-        load_table(beta_table, beta_slots, "beta_table", 0)
+        load_table(beta_table, beta_slots, "beta_table", 1)
 
         nc.vector.tensor_copy(out=w_dst[:, W_SPLIT:P], in_=w_src[:, W_SPLIT:P])
-        load_table(beta_table, beta_slots, "beta_table", 1)
-        for t in EARLY:
+        for t in range(LAST):
             load_table(gamma_table, gamma_slots, "gamma_table", t)
         w_codes = keep.tile([P, N], U32, name="w_codes", align_bytes=64)
         w_scales = keep.tile([P, N], U8, name="w_scales", align_bytes=64)
@@ -97,9 +98,9 @@ def tile_picked_cbn_none_po_kernel(tc, x_words, x_scales, w1, gamma, beta, offs,
 
         picked_words = keep.tile([P, S], U32, name="picked_words", tag="w_bf_then_picked_words", align_bytes=64)
         nc.vector.tensor_copy(out=picked_words[:], in_=x_word_table[:].bitcast(U32).indirect(offs_t[:]))
+        load_table(gamma_table, gamma_slots, "gamma_table", LAST)
         for t in LATE:
-            load_table(gamma_table, gamma_slots, "gamma_table", t)
-        load_table(beta_table, beta_slots, "beta_table", LATE[0])
+            load_table(beta_table, beta_slots, "beta_table", t)
 
         picked_beta = keep.tile([P, len(EARLY), S], F32, name="picked_beta", align_bytes=64)
         y = keep.tile([P, PACK, S], F32, name="y", align_bytes=64)
@@ -131,10 +132,8 @@ def tile_picked_cbn_none_po_kernel(tc, x_words, x_scales, w1, gamma, beta, offs,
         sums = {}
         for t in EARLY:
             nc.vector.tensor_copy(out=picked_beta[:, t, :], in_=beta_table[t][:].indirect(cls_t[:]))
-            if t == 0:
-                load_table(beta_table, beta_slots, "beta_table", LAST)
             for lo in HALVES:
-                sums[t, lo] = psum.tile([P, HALF], F32, name=f"sum{t}_{lo}")
+                sums[t, lo] = psum.tile([P, HALF], F32, name=f"sum{t}_{lo}", tag=f"bank{2 * t + lo // HALF}")
                 turn(sums[t, lo], picked_beta[:, t, :], lo, True, False)
         for t in range(PACK):
             nc.vector.tensor_tensor(out=scaled[:, t, :], in0=gamma_table[t][:].indirect(cls_t[:]), in1=y[:, t, :], op=MULT)
@@ -142,8 +141,8 @@ def tile_picked_cbn_none_po_kernel(tc, x_words, x_scales, w1, gamma, beta, offs,
             for lo in HALVES:
                 turn(sums[t, lo], scaled[:, t, :], lo, False, True)
                 nc.scalar.copy(out=turned[:, t, lo : lo + HALF], in_=sums[t, lo][:])
-            for h, lo in enumerate(HALVES):
-                back = psum.tile([P, HALF], F32, name=f"back{t}_{lo}", tag=f"bank{2 * t + h}")
+            for lo in HALVES:
+                back = psum.tile([P, HALF], F32, name=f"back{t}_{lo}")
                 turn(back, turned[:, t, :], lo, True, True)
                 nc.scalar.copy(out=result[:, t, lo : lo + HALF], in_=back[:])
         nc.sync.dma_start(out=out_slots[:, 0:2, :], in_=result[:, 0:2, :])

@@ -26,12 +26,11 @@ HALF = S // 2
 HALVES = (0, HALF)
 LAST = PACK - 1
 EARLY, LATE = (0, 1), (2, 3)
-BLOCKS = HALF // P
 TABLE_BYTES = 4 * U
 RING = 8
 LANDING = 16
 W_SPLIT = 48
-ROUND_SPLITS = (HALF // 2, HALF + HALF // 4)
+ROUND_SPLITS = (HALF // 2, HALF + 3 * HALF // 8)
 
 
 def tile_picked_cbn_none_po_kernel(tc, x_words, x_scales, w1, gamma, beta, offs, cls, out_0, out_1, out_2):
@@ -122,9 +121,7 @@ def tile_picked_cbn_none_po_kernel(tc, x_words, x_scales, w1, gamma, beta, offs,
             nc.scalar.copy(out=y[:, t, :], in_=acc[:])
 
         def turn(bank, source, lo, start, stop):
-            for i in range(BLOCKS):
-                cols = slice(lo + i * P, lo + (i + 1) * P)
-                nc.tensor.matmul(out=bank[:, i * P : (i + 1) * P], lhsT=source[:, cols], rhs=identity[:], is_transpose=True, start=start and i == 0, stop=stop and i == BLOCKS - 1)
+            nc.tensor.matmul(out=bank[:], lhsT=source[:, lo : lo + P], rhs=identity[:], is_transpose=True, start=start, stop=stop)
 
         def add_beta(t, lo, hi):
             nc.vector.tensor_tensor(out=result[:, t, lo:hi], in0=beta_table[t][:].indirect(entries(cls_t, lo, hi)), in1=scaled[:, t, lo:hi], op=ADD)
@@ -132,19 +129,19 @@ def tile_picked_cbn_none_po_kernel(tc, x_words, x_scales, w1, gamma, beta, offs,
         sums = {}
         for t in EARLY:
             nc.vector.tensor_copy(out=picked_beta[:, t, :], in_=beta_table[t][:].indirect(cls_t[:]))
-            for lo in HALVES:
-                sums[t, lo] = psum.tile([P, HALF], F32, name=f"sum{t}_{lo}", tag=f"bank{2 * t + lo // HALF}")
+            for lo in range(0, S, P):
+                sums[t, lo] = psum.tile([P, P], F32, name=f"sum{t}_{lo}", tag=f"bank{PACK * t + lo // P}")
                 turn(sums[t, lo], picked_beta[:, t, :], lo, True, False)
         for t in range(PACK):
             nc.vector.tensor_tensor(out=scaled[:, t, :], in0=gamma_table[t][:].indirect(cls_t[:]), in1=y[:, t, :], op=MULT)
         for t in EARLY:
-            for lo in HALVES:
+            for lo in range(0, S, P):
                 turn(sums[t, lo], scaled[:, t, :], lo, False, True)
-                nc.scalar.copy(out=turned[:, t, lo : lo + HALF], in_=sums[t, lo][:])
-            for lo in HALVES:
-                back = psum.tile([P, HALF], F32, name=f"back{t}_{lo}")
+                nc.scalar.copy(out=turned[:, t, lo : lo + P], in_=sums[t, lo][:])
+            for lo in range(0, S, P):
+                back = psum.tile([P, P], F32, name=f"back{t}_{lo}", tag=f"bank{PACK * t + lo // P}")
                 turn(back, turned[:, t, :], lo, True, True)
-                nc.scalar.copy(out=result[:, t, lo : lo + HALF], in_=back[:])
+                nc.scalar.copy(out=result[:, t, lo : lo + P], in_=back[:])
         nc.sync.dma_start(out=out_slots[:, 0:2, :], in_=result[:, 0:2, :])
         add_beta(2, 0, S)
         nc.sync.dma_start(out=out_slots[:, 2, :], in_=result[:, 2, :])

@@ -24,20 +24,23 @@ QUADRANTS = P // QUADRANT
 LIST_ROWS = 16
 HALF = S // 2
 HALVES = (0, HALF)
+QUARTER = S // 4
 LAST = PACK - 1
 EARLY, LATE = (0, 1), (2, 3)
-TABLE_BYTES = 4 * U
-RING = 8
 LANDING = 16
+TABLE_BYTES = 4 * U
+SCALE_PLACE = 0
+W_PLACES = (1, 2, 3)
+X_PLACES = (4, 5, 6)
+FREE_PLACE = 7
 W_SPLIT = 48
-ROUND_SPLITS = (HALF // 2, HALF + 3 * HALF // 8)
 
 
 def tile_picked_cbn_none_po_kernel(tc, x_words, x_scales, w1, gamma, beta, offs, cls, out_0, out_1, out_2):
     nc = tc.nc
     with ExitStack() as ctx:
         keep = ctx.enter_context(tc.tile_pool(name="keep", bufs=1))
-        ring = ctx.enter_context(tc.tile_pool(name="ring", bufs=1))
+        shared = ctx.enter_context(tc.tile_pool(name="tables", bufs=1))
         psum = ctx.enter_context(tc.psum_pool(name="psum", bufs=1))
 
         def entries(list_tile, lo, hi):
@@ -48,9 +51,9 @@ def tile_picked_cbn_none_po_kernel(tc, x_words, x_scales, w1, gamma, beta, offs,
 
         offs_t = keep.tile([P, S // LIST_ROWS], U16, name="offs_t")
         cls_t = keep.tile([P, S // LIST_ROWS], U16, name="cls_t")
-        x_word_table = ring.tile([P, T], I32, name="x_word_table", offset=4 * TABLE_BYTES + TABLE_BYTES // 2)
-        x_scale_table = ring.tile([P, T], U8, name="x_scale_table", offset=0)
-        w_raw = ring.tile([P, PACK, N], F32, name="w_raw", offset=TABLE_BYTES + TABLE_BYTES // 2)
+        x_word_table = shared.tile([P, T], I32, name="x_word_table", offset=X_PLACES[0] * TABLE_BYTES + TABLE_BYTES // 2)
+        x_scale_table = shared.tile([P, T], U8, name="x_scale_table", offset=SCALE_PLACE * TABLE_BYTES)
+        w_raw = shared.tile([P, PACK, N], F32, name="w_raw", offset=W_PLACES[0] * TABLE_BYTES + TABLE_BYTES // 2)
         gamma_table, beta_table = {}, {}
 
         gamma_slots = gamma.rearrange("(p t) u -> p t u", t=PACK)
@@ -62,17 +65,21 @@ def tile_picked_cbn_none_po_kernel(tc, x_words, x_scales, w1, gamma, beta, offs,
             nc.vector.memset(x_scale_table[lo:hi, :].bitcast(I32), 0)
         picked_scales = keep.tile([P, S], U8, name="picked_scales", align_bytes=64)
         nc.vector.memset(picked_scales[:].bitcast(I32), 0)
+
         nc.sync.dma_start(out=offs_t[:], in_=offs)
         nc.sync.dma_start(out=w_raw[:], in_=w1.rearrange("(p r) c -> p r c", r=PACK))
         nc.sync.dma_start(out=x_word_table[:], in_=x_words[0].rearrange("p c r -> p (c r)").bitcast(I32))
         nc.sync.dma_start(out=cls_t[:], in_=cls)
 
-        def load_table(tables, slots, name, t):
-            place = (len(gamma_table) + len(beta_table) - 1) % RING
-            tables[t] = ring.tile([P, U], F32, name=f"{name}{t}", offset=place * TABLE_BYTES)
-            nc.sync.dma_start(out=tables[t][:], in_=slots[:, t, :])
+        def load_gamma(t, place):
+            gamma_table[t] = shared.tile([P, U], F32, name=f"gamma_table{t}", offset=place * TABLE_BYTES)
+            nc.sync.dma_start(out=gamma_table[t][:], in_=gamma_slots[:, t, :])
 
-        load_table(beta_table, beta_slots, "beta_table", 0)
+        def load_beta(t, place):
+            beta_table[t] = shared.tile([P, U], F32, name=f"beta_table{t}", offset=place * TABLE_BYTES)
+            nc.sync.dma_start(out=beta_table[t][:], in_=beta_slots[:, t, :])
+
+        load_beta(EARLY[0], FREE_PLACE)
 
         identity = keep.tile([P, P], F32, name="identity")
         make_identity(nc, identity[:])
@@ -86,20 +93,20 @@ def tile_picked_cbn_none_po_kernel(tc, x_words, x_scales, w1, gamma, beta, offs,
         nc.vector.tensor_copy(out=picked_landing[:], in_=x_scale_table[:].indirect(offs_t[:]))
         for r in range(SCALE_ROWS):
             nc.sync.dma_start(out=picked_scales[r:P:QUADRANT, :].bitcast(I32), in_=picked_landing[LANDING + r : QUADRANT : SCALE_ROWS, :].bitcast(I32))
-        load_table(beta_table, beta_slots, "beta_table", 1)
+        load_beta(EARLY[1], SCALE_PLACE)
 
         nc.vector.tensor_copy(out=w_dst[:, W_SPLIT:P], in_=w_src[:, W_SPLIT:P])
-        for t in range(LAST):
-            load_table(gamma_table, gamma_slots, "gamma_table", t)
+        for t, place in enumerate(W_PLACES):
+            load_gamma(t, place)
         w_codes = keep.tile([P, N], U32, name="w_codes", align_bytes=64)
         w_scales = keep.tile([P, N], U8, name="w_scales", align_bytes=64)
         nc.vector.quantize_mx(out=w_codes[:].bitcast(FP8X4), scales=w_scales[:], in_=w_bf[:].rearrange("p t m r -> p (t m r)"))
 
         picked_words = keep.tile([P, S], U32, name="picked_words", tag="w_bf_then_picked_words", align_bytes=64)
         nc.vector.tensor_copy(out=picked_words[:], in_=x_word_table[:].bitcast(U32).indirect(offs_t[:]))
-        load_table(gamma_table, gamma_slots, "gamma_table", LAST)
-        for t in LATE:
-            load_table(beta_table, beta_slots, "beta_table", t)
+        load_gamma(LAST, X_PLACES[0])
+        for t, place in zip(LATE, X_PLACES[1:]):
+            load_beta(t, place)
 
         picked_beta = keep.tile([P, len(EARLY), S], F32, name="picked_beta", align_bytes=64)
         y = keep.tile([P, PACK, S], F32, name="y", align_bytes=64)
@@ -123,6 +130,9 @@ def tile_picked_cbn_none_po_kernel(tc, x_words, x_scales, w1, gamma, beta, offs,
         def turn(bank, source, lo, start, stop):
             nc.tensor.matmul(out=bank[:], lhsT=source[:, lo : lo + P], rhs=identity[:], is_transpose=True, start=start, stop=stop)
 
+        def sum_bank(t, lo):
+            return f"bank{(S // P) * t + lo // P}"
+
         def add_beta(t, lo, hi):
             nc.vector.tensor_tensor(out=result[:, t, lo:hi], in0=beta_table[t][:].indirect(entries(cls_t, lo, hi)), in1=scaled[:, t, lo:hi], op=ADD)
 
@@ -130,7 +140,7 @@ def tile_picked_cbn_none_po_kernel(tc, x_words, x_scales, w1, gamma, beta, offs,
         for t in EARLY:
             nc.vector.tensor_copy(out=picked_beta[:, t, :], in_=beta_table[t][:].indirect(cls_t[:]))
             for lo in range(0, S, P):
-                sums[t, lo] = psum.tile([P, P], F32, name=f"sum{t}_{lo}", tag=f"bank{PACK * t + lo // P}")
+                sums[t, lo] = psum.tile([P, P], F32, name=f"sum{t}_{lo}", tag=sum_bank(t, lo))
                 turn(sums[t, lo], picked_beta[:, t, :], lo, True, False)
         for t in range(PACK):
             nc.vector.tensor_tensor(out=scaled[:, t, :], in0=gamma_table[t][:].indirect(cls_t[:]), in1=y[:, t, :], op=MULT)
@@ -139,12 +149,12 @@ def tile_picked_cbn_none_po_kernel(tc, x_words, x_scales, w1, gamma, beta, offs,
                 turn(sums[t, lo], scaled[:, t, :], lo, False, True)
                 nc.scalar.copy(out=turned[:, t, lo : lo + P], in_=sums[t, lo][:])
             for lo in range(0, S, P):
-                back = psum.tile([P, P], F32, name=f"back{t}_{lo}", tag=f"bank{PACK * t + lo // P}")
+                back = psum.tile([P, P], F32, name=f"back{t}_{lo}", tag=sum_bank(t, lo))
                 turn(back, turned[:, t, :], lo, True, True)
                 nc.scalar.copy(out=result[:, t, lo : lo + P], in_=back[:])
-        nc.sync.dma_start(out=out_slots[:, 0:2, :], in_=result[:, 0:2, :])
-        add_beta(2, 0, S)
-        nc.sync.dma_start(out=out_slots[:, 2, :], in_=result[:, 2, :])
+        nc.sync.dma_start(out=out_slots[:, 0 : len(EARLY), :], in_=result[:, 0 : len(EARLY), :])
+        add_beta(LATE[0], 0, S)
+        nc.sync.dma_start(out=out_slots[:, LATE[0], :], in_=result[:, LATE[0], :])
 
         rounded = [keep.tile([P, HALF, PACK], BF16, name=f"rounded{h}", align_bytes=64) for h in range(len(HALVES))]
         out_codes = keep.tile([P, S], I32, name="out_codes", align_bytes=64)
@@ -155,21 +165,22 @@ def tile_picked_cbn_none_po_kernel(tc, x_words, x_scales, w1, gamma, beta, offs,
             h = lo // HALF
             copy(out=rounded[h][:, lo - HALVES[h] : hi - HALVES[h], t : t + 2], in_=result[:, t : t + 2, lo:hi].rearrange("p t c -> p c t"))
 
-        def quantise_half(h):
-            cols = slice(HALVES[h], HALVES[h] + HALF)
-            nc.vector.quantize_mx(out=out_codes[:, cols].bitcast(FP8X4), scales=out_scales[:, cols], in_=rounded[h][:].rearrange("p c t -> p (c t)"))
-            nc.sync.dma_start(out=out_words[:, cols], in_=out_codes[:, cols])
+        def quantise(lo, hi):
+            h = lo // HALF
+            source = rounded[h][:, lo - HALVES[h] : hi - HALVES[h], :].rearrange("p c t -> p (c t)")
+            nc.vector.quantize_mx(out=out_codes[:, lo:hi].bitcast(FP8X4), scales=out_scales[:, lo:hi], in_=source)
+            nc.sync.dma_start(out=out_words[:, lo:hi], in_=out_codes[:, lo:hi])
 
         for lo in HALVES:
-            round_pair(nc.scalar.copy, 0, lo, lo + HALF)
+            round_pair(nc.scalar.copy, EARLY[0], lo, lo + HALF)
         add_beta(LAST, 0, HALF)
         add_beta(LAST, HALF, S)
         nc.sync.dma_start(out=out_slots[:, LAST, :], in_=result[:, LAST, :])
-        for lo, split in zip(HALVES, ROUND_SPLITS):
-            round_pair(nc.scalar.copy, 2, lo, split)
-            round_pair(nc.vector.tensor_copy, 2, split, lo + HALF)
-        for h in range(len(HALVES)):
-            quantise_half(h)
+        for copy, lo in zip((nc.scalar.copy, nc.vector.tensor_copy, nc.vector.tensor_copy, nc.scalar.copy), range(0, S, QUARTER)):
+            round_pair(copy, LATE[0], lo, lo + QUARTER)
+        quantise(0, HALF)
+        quantise(HALF, S - QUARTER)
+        quantise(S - QUARTER, S)
 
         for q in range(QUADRANTS):
             queue = nc.scalar if q % 2 == 0 else nc.sync

@@ -1,7 +1,6 @@
 from contextlib import ExitStack
 
 import concourse.mybir as mybir
-from concourse.masks import make_identity
 
 K, T, S, N, U = 512, 2048, 512, 512, 1024
 FLOPS = 2 * K * N * S
@@ -15,6 +14,7 @@ U8 = mybir.dt.uint8
 FP8X4 = mybir.dt.float8_e4m3fn_x4
 MULT = mybir.AluOpType.mult
 ADD = mybir.AluOpType.add
+COPY = mybir.ActivationFunctionType.Copy
 
 P = 128
 PACK = 4
@@ -23,17 +23,15 @@ SCALE_ROWS = 4
 QUADRANTS = P // QUADRANT
 LIST_ROWS = 16
 HALF = S // 2
-HALVES = (0, HALF)
 QUARTER = S // 4
 LAST = PACK - 1
-EARLY, LATE = (0, 1), (2, 3)
 LANDING = 16
 TABLE_BYTES = 4 * U
-SCALE_PLACE = 0
-W_PLACES = (1, 2, 3)
-X_PLACES = (4, 5, 6)
-FREE_PLACE = 7
+SCALE_OFFSET = TABLE_BYTES - T // 2
+W_OFFSET = 2 * TABLE_BYTES + TABLE_BYTES // 2
+X_OFFSET = 5 * TABLE_BYTES + TABLE_BYTES // 2
 W_SPLIT = 48
+GAMMA_SPLIT = 192
 
 
 def tile_picked_cbn_none_po_kernel(tc, x_words, x_scales, w1, gamma, beta, offs, cls, out_0, out_1, out_2):
@@ -51,9 +49,9 @@ def tile_picked_cbn_none_po_kernel(tc, x_words, x_scales, w1, gamma, beta, offs,
 
         offs_t = keep.tile([P, S // LIST_ROWS], U16, name="offs_t")
         cls_t = keep.tile([P, S // LIST_ROWS], U16, name="cls_t")
-        x_word_table = shared.tile([P, T], I32, name="x_word_table", offset=X_PLACES[0] * TABLE_BYTES + TABLE_BYTES // 2)
-        x_scale_table = shared.tile([P, T], U8, name="x_scale_table", offset=SCALE_PLACE * TABLE_BYTES)
-        w_raw = shared.tile([P, PACK, N], F32, name="w_raw", offset=W_PLACES[0] * TABLE_BYTES + TABLE_BYTES // 2)
+        x_word_table = shared.tile([P, T], I32, name="x_word_table", offset=X_OFFSET)
+        x_scale_table = shared.tile([P, T], U8, name="x_scale_table", offset=SCALE_OFFSET)
+        w_raw = shared.tile([P, PACK, N], F32, name="w_raw", offset=W_OFFSET)
         gamma_table, beta_table = {}, {}
 
         gamma_slots = gamma.rearrange("(p t) u -> p t u", t=PACK)
@@ -79,11 +77,6 @@ def tile_picked_cbn_none_po_kernel(tc, x_words, x_scales, w1, gamma, beta, offs,
             beta_table[t] = shared.tile([P, U], F32, name=f"beta_table{t}", offset=place * TABLE_BYTES)
             nc.sync.dma_start(out=beta_table[t][:], in_=beta_slots[:, t, :])
 
-        load_beta(EARLY[0], FREE_PLACE)
-
-        identity = keep.tile([P, P], F32, name="identity")
-        make_identity(nc, identity[:])
-
         w_bf = keep.tile([P, PACK, P, PACK], BF16, name="w_bf", tag="w_bf_then_picked_words", align_bytes=64)
         w_dst = w_bf[:].rearrange("p t m r -> p m r t")
         w_src = w_raw[:].rearrange("p r (m t) -> p m r t", t=PACK)
@@ -93,31 +86,26 @@ def tile_picked_cbn_none_po_kernel(tc, x_words, x_scales, w1, gamma, beta, offs,
         nc.vector.tensor_copy(out=picked_landing[:], in_=x_scale_table[:].indirect(offs_t[:]))
         for r in range(SCALE_ROWS):
             nc.sync.dma_start(out=picked_scales[r:P:QUADRANT, :].bitcast(I32), in_=picked_landing[LANDING + r : QUADRANT : SCALE_ROWS, :].bitcast(I32))
-        load_beta(EARLY[1], SCALE_PLACE)
+        load_gamma(0, 0)
+        load_gamma(1, 1)
 
         nc.vector.tensor_copy(out=w_dst[:, W_SPLIT:P], in_=w_src[:, W_SPLIT:P])
-        for t, place in enumerate(W_PLACES):
-            load_gamma(t, place)
+        load_gamma(2, 2)
+        load_gamma(3, 3)
+        load_beta(0, 4)
         w_codes = keep.tile([P, N], U32, name="w_codes", align_bytes=64)
         w_scales = keep.tile([P, N], U8, name="w_scales", align_bytes=64)
         nc.vector.quantize_mx(out=w_codes[:].bitcast(FP8X4), scales=w_scales[:], in_=w_bf[:].rearrange("p t m r -> p (t m r)"))
 
         picked_words = keep.tile([P, S], U32, name="picked_words", tag="w_bf_then_picked_words", align_bytes=64)
         nc.vector.tensor_copy(out=picked_words[:], in_=x_word_table[:].bitcast(U32).indirect(offs_t[:]))
-        load_gamma(LAST, X_PLACES[0])
-        for t, place in zip(LATE, X_PLACES[1:]):
-            load_beta(t, place)
+        for t in (1, 2, 3):
+            load_beta(t, 4 + t)
 
-        picked_beta = keep.tile([P, len(EARLY), S], F32, name="picked_beta", align_bytes=64)
-        y = keep.tile([P, PACK, S], F32, name="y", align_bytes=64)
-        scaled = keep.tile([P, PACK, S], F32, name="scaled", align_bytes=64)
-        turned = keep.tile([P, len(EARLY), S], F32, name="turned", align_bytes=64)
-        result = keep.tile([P, PACK, S], F32, name="result", align_bytes=64)
-
+        acc = [psum.tile([P, S], F32, name=f"acc{t}") for t in range(PACK)]
         for t in range(PACK):
-            acc = psum.tile([P, S], F32, name=f"acc{t}", tag=f"bank{t}")
             nc.tensor.matmul_mx(
-                out=acc[:],
+                out=acc[t][:],
                 lhsT=w_codes[:, t * P : (t + 1) * P].bitcast(FP8X4),
                 lhsT_scale=w_scales[:, t * P : (t + 1) * P],
                 rhs=picked_words[:].bitcast(FP8X4),
@@ -125,62 +113,70 @@ def tile_picked_cbn_none_po_kernel(tc, x_words, x_scales, w1, gamma, beta, offs,
                 start=True,
                 stop=True,
             )
-            nc.scalar.copy(out=y[:, t, :], in_=acc[:])
 
-        def turn(bank, source, lo, start, stop):
-            nc.tensor.matmul(out=bank[:], lhsT=source[:, lo : lo + P], rhs=identity[:], is_transpose=True, start=start, stop=stop)
+        scaled = [keep.tile([P, S], F32, name=f"scaled{t}", align_bytes=64) for t in range(PACK)]
+        result = keep.tile([P, PACK, S], F32, name="result", align_bytes=64)
 
-        def sum_bank(t, lo):
-            return f"bank{(S // P) * t + lo // P}"
+        def look_up(picked, table, lo):
+            nc.scalar.activation(out=picked, in_=table[:].indirect(entries(cls_t, lo, S)), func=COPY)
 
-        def add_beta(t, lo, hi):
-            nc.vector.tensor_tensor(out=result[:, t, lo:hi], in0=beta_table[t][:].indirect(entries(cls_t, lo, hi)), in1=scaled[:, t, lo:hi], op=ADD)
-
-        sums = {}
-        for t in EARLY:
-            nc.vector.tensor_copy(out=picked_beta[:, t, :], in_=beta_table[t][:].indirect(cls_t[:]))
-            for lo in range(0, S, P):
-                sums[t, lo] = psum.tile([P, P], F32, name=f"sum{t}_{lo}", tag=sum_bank(t, lo))
-                turn(sums[t, lo], picked_beta[:, t, :], lo, True, False)
         for t in range(PACK):
-            nc.vector.tensor_tensor(out=scaled[:, t, :], in0=gamma_table[t][:].indirect(cls_t[:]), in1=y[:, t, :], op=MULT)
-        for t in EARLY:
-            for lo in range(0, S, P):
-                turn(sums[t, lo], scaled[:, t, :], lo, False, True)
-                nc.scalar.copy(out=turned[:, t, lo : lo + P], in_=sums[t, lo][:])
-            for lo in range(0, S, P):
-                back = psum.tile([P, P], F32, name=f"back{t}_{lo}", tag=sum_bank(t, lo))
-                turn(back, turned[:, t, :], lo, True, True)
-                nc.scalar.copy(out=result[:, t, lo : lo + P], in_=back[:])
-        nc.sync.dma_start(out=out_slots[:, 0 : len(EARLY), :], in_=result[:, 0 : len(EARLY), :])
-        add_beta(LATE[0], 0, S)
-        nc.sync.dma_start(out=out_slots[:, LATE[0], :], in_=result[:, LATE[0], :])
+            picked_gamma = keep.tile([P, S], F32, name=f"picked_gamma{t}", align_bytes=64)
+            look_up(picked_gamma[:, GAMMA_SPLIT:S], gamma_table[t], GAMMA_SPLIT)
+            nc.vector.tensor_copy(out=picked_gamma[:, 0:GAMMA_SPLIT], in_=gamma_table[t][:].indirect(entries(cls_t, 0, GAMMA_SPLIT)))
+            for lo, hi in ((GAMMA_SPLIT, S), (0, GAMMA_SPLIT)):
+                nc.vector.tensor_tensor(out=scaled[t][:, lo:hi], in0=acc[t][:, lo:hi], in1=picked_gamma[:, lo:hi], op=MULT)
 
-        rounded = [keep.tile([P, HALF, PACK], BF16, name=f"rounded{h}", align_bytes=64) for h in range(len(HALVES))]
+        picked_beta = [keep.tile([P, HALF], F32, name=f"picked_beta{t}", align_bytes=64) for t in range(PACK)]
+
+        def add_fused(t, lo, hi):
+            nc.vector.tensor_tensor(out=result[:, t, lo:hi], in0=beta_table[t][:].indirect(entries(cls_t, lo, hi)), in1=scaled[t][:, lo:hi], op=ADD)
+
+        def add_picked(t):
+            nc.vector.tensor_tensor(out=result[:, t, HALF:S], in0=picked_beta[t][:], in1=scaled[t][:, HALF:S], op=ADD)
+
+        for t in range(LAST):
+            look_up(picked_beta[t][:], beta_table[t], HALF)
+            add_fused(t, 0, HALF)
+            add_picked(t)
+            if t == 1:
+                nc.sync.dma_start(out=out_slots[:, 0:2, :], in_=result[:, 0:2, :])
+        nc.sync.dma_start(out=out_slots[:, 2, :], in_=result[:, 2, :])
+
+        rounded = [keep.tile([P, QUARTER, PACK], BF16, name=f"rounded{q}", align_bytes=64) for q in range(S // QUARTER)]
         out_codes = keep.tile([P, S], I32, name="out_codes", align_bytes=64)
         out_scales = keep.tile([P, S], U8, name="out_scales", align_bytes=64)
         out_words = out_1[0].rearrange("p c r -> p (c r)").bitcast(I32)
 
-        def round_pair(copy, t, lo, hi):
-            h = lo // HALF
-            copy(out=rounded[h][:, lo - HALVES[h] : hi - HALVES[h], t : t + 2], in_=result[:, t : t + 2, lo:hi].rearrange("p t c -> p c t"))
+        def round_quarter(copy, q):
+            copy(
+                out=rounded[q][:].rearrange("p (c i) t -> p c t i", i=PACK),
+                in_=result[:, :, q * QUARTER : (q + 1) * QUARTER].rearrange("p t (c i) -> p c t i", i=PACK),
+            )
 
-        def quantise(lo, hi):
-            h = lo // HALF
-            source = rounded[h][:, lo - HALVES[h] : hi - HALVES[h], :].rearrange("p c t -> p (c t)")
-            nc.vector.quantize_mx(out=out_codes[:, lo:hi].bitcast(FP8X4), scales=out_scales[:, lo:hi], in_=source)
+        def quantise(q):
+            columns = slice(q * QUARTER, (q + 1) * QUARTER)
+            nc.vector.quantize_mx(out=out_codes[:, columns].bitcast(FP8X4), scales=out_scales[:, columns], in_=rounded[q][:].rearrange("p c t -> p (c t)"))
+
+        def store_words(lo, hi):
             nc.sync.dma_start(out=out_words[:, lo:hi], in_=out_codes[:, lo:hi])
 
-        for lo in HALVES:
-            round_pair(nc.scalar.copy, EARLY[0], lo, lo + HALF)
-        add_beta(LAST, 0, HALF)
-        add_beta(LAST, HALF, S)
+        look_up(picked_beta[LAST][:], beta_table[LAST], HALF)
+        add_fused(LAST, 0, QUARTER)
+        add_fused(LAST, QUARTER, HALF)
+        round_quarter(nc.vector.tensor_copy, 0)
+        round_quarter(nc.scalar.copy, 1)
+        add_picked(LAST)
         nc.sync.dma_start(out=out_slots[:, LAST, :], in_=result[:, LAST, :])
-        for copy, lo in zip((nc.scalar.copy, nc.vector.tensor_copy, nc.vector.tensor_copy, nc.scalar.copy), range(0, S, QUARTER)):
-            round_pair(copy, LATE[0], lo, lo + QUARTER)
-        quantise(0, HALF)
-        quantise(HALF, S - QUARTER)
-        quantise(S - QUARTER, S)
+        quantise(0)
+        round_quarter(nc.vector.tensor_copy, 2)
+        round_quarter(nc.scalar.copy, 3)
+        quantise(1)
+        store_words(0, HALF)
+        quantise(2)
+        store_words(HALF, S - QUARTER)
+        quantise(3)
+        store_words(S - QUARTER, S)
 
         for q in range(QUADRANTS):
             queue = nc.scalar if q % 2 == 0 else nc.sync

@@ -31,7 +31,9 @@ SCALE_OFFSET = TABLE_BYTES - T // 2
 W_OFFSET = 2 * TABLE_BYTES + TABLE_BYTES // 2
 X_OFFSET = 5 * TABLE_BYTES + TABLE_BYTES // 2
 W_SPLIT = 48
-GAMMA_SPLIT = 192
+BY_HALVES = ((0, HALF), (HALF, S))
+ONE_QUARTER = ((0, QUARTER), (QUARTER, QUARTER + HALF), (QUARTER + HALF, S))
+GAMMA_PARTS = (BY_HALVES, BY_HALVES, ONE_QUARTER, ONE_QUARTER)
 
 
 def tile_picked_cbn_none_po_kernel(tc, x_words, x_scales, w1, gamma, beta, offs, cls, out_0, out_1, out_2):
@@ -117,14 +119,15 @@ def tile_picked_cbn_none_po_kernel(tc, x_words, x_scales, w1, gamma, beta, offs,
         scaled = [keep.tile([P, S], F32, name=f"scaled{t}", align_bytes=64) for t in range(PACK)]
         result = keep.tile([P, PACK, S], F32, name="result", align_bytes=64)
 
-        def look_up(picked, table, lo):
-            nc.scalar.activation(out=picked, in_=table[:].indirect(entries(cls_t, lo, S)), func=COPY)
+        def look_up(picked, table, lo, hi):
+            nc.scalar.activation(out=picked, in_=table[:].indirect(entries(cls_t, lo, hi)), func=COPY)
 
-        for t in range(PACK):
+        for t, (own, *others) in enumerate(GAMMA_PARTS):
             picked_gamma = keep.tile([P, S], F32, name=f"picked_gamma{t}", align_bytes=64)
-            look_up(picked_gamma[:, GAMMA_SPLIT:S], gamma_table[t], GAMMA_SPLIT)
-            nc.vector.tensor_copy(out=picked_gamma[:, 0:GAMMA_SPLIT], in_=gamma_table[t][:].indirect(entries(cls_t, 0, GAMMA_SPLIT)))
-            for lo, hi in ((GAMMA_SPLIT, S), (0, GAMMA_SPLIT)):
+            for lo, hi in others:
+                look_up(picked_gamma[:, lo:hi], gamma_table[t], lo, hi)
+            nc.vector.tensor_copy(out=picked_gamma[:, own[0] : own[1]], in_=gamma_table[t][:].indirect(entries(cls_t, *own)))
+            for lo, hi in (others[0], own, *others[1:]):
                 nc.vector.tensor_tensor(out=scaled[t][:, lo:hi], in0=acc[t][:, lo:hi], in1=picked_gamma[:, lo:hi], op=MULT)
 
         picked_beta = [keep.tile([P, HALF], F32, name=f"picked_beta{t}", align_bytes=64) for t in range(PACK)]
@@ -136,7 +139,7 @@ def tile_picked_cbn_none_po_kernel(tc, x_words, x_scales, w1, gamma, beta, offs,
             nc.vector.tensor_tensor(out=result[:, t, HALF:S], in0=picked_beta[t][:], in1=scaled[t][:, HALF:S], op=ADD)
 
         for t in range(LAST):
-            look_up(picked_beta[t][:], beta_table[t], HALF)
+            look_up(picked_beta[t][:], beta_table[t], HALF, S)
             add_fused(t, 0, HALF)
             add_picked(t)
             if t == 1:
@@ -161,7 +164,7 @@ def tile_picked_cbn_none_po_kernel(tc, x_words, x_scales, w1, gamma, beta, offs,
         def store_words(lo, hi):
             nc.sync.dma_start(out=out_words[:, lo:hi], in_=out_codes[:, lo:hi])
 
-        look_up(picked_beta[LAST][:], beta_table[LAST], HALF)
+        look_up(picked_beta[LAST][:], beta_table[LAST], HALF, S)
         add_fused(LAST, 0, QUARTER)
         add_fused(LAST, QUARTER, HALF)
         round_quarter(nc.vector.tensor_copy, 0)

@@ -31,9 +31,10 @@ SCALE_OFFSET = TABLE_BYTES - T // 2
 W_OFFSET = 2 * TABLE_BYTES + TABLE_BYTES // 2
 X_OFFSET = 5 * TABLE_BYTES + TABLE_BYTES // 2
 W_SPLIT = 48
+THREE_QUARTERS = ((0, S - QUARTER), (S - QUARTER, S))
 BY_HALVES = ((0, HALF), (HALF, S))
 ONE_QUARTER = ((0, QUARTER), (QUARTER, QUARTER + HALF), (QUARTER + HALF, S))
-GAMMA_PARTS = (BY_HALVES, BY_HALVES, ONE_QUARTER, ONE_QUARTER)
+GAMMA_PARTS = (THREE_QUARTERS, BY_HALVES, BY_HALVES, ONE_QUARTER)
 
 
 def tile_picked_cbn_none_po_kernel(tc, x_words, x_scales, w1, gamma, beta, offs, cls, out_0, out_1, out_2):

@@ -26,6 +26,7 @@ HALF = S // 2
 QUARTER = S // 4
 LAST = PACK - 1
 LANDING = 16
+DMA_ALIGN = 256
 TABLE_BYTES = 4 * U
 SCALE_OFFSET = TABLE_BYTES - T // 2
 W_OFFSET = 2 * TABLE_BYTES + TABLE_BYTES // 2
@@ -52,9 +53,9 @@ def tile_picked_cbn_none_po_kernel(tc, x_words, x_scales, w1, gamma, beta, offs,
 
         offs_t = keep.tile([P, S // LIST_ROWS], U16, name="offs_t")
         cls_t = keep.tile([P, S // LIST_ROWS], U16, name="cls_t")
-        x_word_table = shared.tile([P, T], I32, name="x_word_table", offset=X_OFFSET)
-        x_scale_table = shared.tile([P, T], U8, name="x_scale_table", offset=SCALE_OFFSET)
-        w_raw = shared.tile([P, PACK, N], F32, name="w_raw", offset=W_OFFSET)
+        x_word_table = shared.tile([P, T], I32, name="x_word_table", align_bytes=DMA_ALIGN, offset=X_OFFSET)
+        x_scale_table = shared.tile([P, T], U8, name="x_scale_table", align_bytes=DMA_ALIGN, offset=SCALE_OFFSET)
+        w_raw = shared.tile([P, PACK, N], F32, name="w_raw", align_bytes=DMA_ALIGN, offset=W_OFFSET)
         gamma_table, beta_table = {}, {}
 
         gamma_slots = gamma.rearrange("(p t) u -> p t u", t=PACK)
@@ -73,11 +74,11 @@ def tile_picked_cbn_none_po_kernel(tc, x_words, x_scales, w1, gamma, beta, offs,
         nc.sync.dma_start(out=cls_t[:], in_=cls)
 
         def load_gamma(t, place):
-            gamma_table[t] = shared.tile([P, U], F32, name=f"gamma_table{t}", offset=place * TABLE_BYTES)
+            gamma_table[t] = shared.tile([P, U], F32, name=f"gamma_table{t}", align_bytes=DMA_ALIGN, offset=place * TABLE_BYTES)
             nc.sync.dma_start(out=gamma_table[t][:], in_=gamma_slots[:, t, :])
 
         def load_beta(t, place):
-            beta_table[t] = shared.tile([P, U], F32, name=f"beta_table{t}", offset=place * TABLE_BYTES)
+            beta_table[t] = shared.tile([P, U], F32, name=f"beta_table{t}", align_bytes=DMA_ALIGN, offset=place * TABLE_BYTES)
             nc.sync.dma_start(out=beta_table[t][:], in_=beta_slots[:, t, :])
 
         w_bf = keep.tile([P, PACK, P, PACK], BF16, name="w_bf", tag="w_bf_then_picked_words", align_bytes=64)
@@ -118,7 +119,7 @@ def tile_picked_cbn_none_po_kernel(tc, x_words, x_scales, w1, gamma, beta, offs,
             )
 
         scaled = [keep.tile([P, S], F32, name=f"scaled{t}", align_bytes=64) for t in range(PACK)]
-        result = keep.tile([P, PACK, S], F32, name="result", align_bytes=64)
+        result = keep.tile([P, PACK, S], F32, name="result", align_bytes=DMA_ALIGN)
 
         def look_up(picked, table, lo, hi):
             nc.scalar.activation(out=picked, in_=table[:].indirect(entries(cls_t, lo, hi)), func=COPY)
@@ -148,8 +149,8 @@ def tile_picked_cbn_none_po_kernel(tc, x_words, x_scales, w1, gamma, beta, offs,
         nc.sync.dma_start(out=out_slots[:, 2, :], in_=result[:, 2, :])
 
         rounded = [keep.tile([P, QUARTER, PACK], BF16, name=f"rounded{q}", align_bytes=64) for q in range(S // QUARTER)]
-        out_codes = keep.tile([P, S], I32, name="out_codes", align_bytes=64)
-        out_scales = keep.tile([P, S], U8, name="out_scales", align_bytes=64)
+        out_codes = keep.tile([P, S], I32, name="out_codes", align_bytes=DMA_ALIGN)
+        out_scales = keep.tile([P, S], U8, name="out_scales", align_bytes=DMA_ALIGN)
         out_words = out_1[0].rearrange("p c r -> p (c r)").bitcast(I32)
 
         def round_quarter(copy, q):

@@ -25,7 +25,7 @@ LIST_ROWS = 16
 HALF = S // 2
 QUARTER = S // 4
 LAST = PACK - 1
-LANDING = 16
+LANDING = 48
 DMA_ALIGN = 256
 TABLE_BYTES = 4 * U
 SCALE_OFFSET = TABLE_BYTES - T // 2
@@ -62,8 +62,8 @@ def tile_picked_cbn_none_po_kernel(tc, x_words, x_scales, w1, gamma, beta, offs,
         beta_slots = beta.rearrange("(p t) u -> p t u", t=PACK)
         out_slots = out_0.rearrange("(p t) s -> p t s", t=PACK)
 
-        nc.scalar.dma_start(out=x_scale_table[LANDING:QUADRANT, :].bitcast(I32), in_=x_scales[0].bitcast(I32))
-        for lo, hi in ((0, LANDING), (QUADRANT, 2 * QUADRANT), (2 * QUADRANT, P)):
+        nc.scalar.dma_start(out=x_scale_table[LANDING : 2 * QUADRANT, :].bitcast(I32), in_=x_scales[0].bitcast(I32))
+        for lo, hi in ((0, LANDING), (2 * QUADRANT, P)):
             nc.vector.memset(x_scale_table[lo:hi, :].bitcast(I32), 0)
         picked_scales = keep.tile([P, S], U8, name="picked_scales", align_bytes=64)
         nc.vector.memset(picked_scales[:].bitcast(I32), 0)
@@ -89,7 +89,7 @@ def tile_picked_cbn_none_po_kernel(tc, x_words, x_scales, w1, gamma, beta, offs,
         picked_landing = keep.tile([P, S], U8, name="picked_landing", align_bytes=64)
         nc.vector.tensor_copy(out=picked_landing[:], in_=x_scale_table[:].indirect(offs_t[:]))
         for r in range(SCALE_ROWS):
-            nc.sync.dma_start(out=picked_scales[r:P:QUADRANT, :].bitcast(I32), in_=picked_landing[LANDING + r : QUADRANT : SCALE_ROWS, :].bitcast(I32))
+            nc.sync.dma_start(out=picked_scales[r:P:QUADRANT, :].bitcast(I32), in_=picked_landing[LANDING + r : 2 * QUADRANT : SCALE_ROWS, :].bitcast(I32))
         load_gamma(0, 0)
         load_gamma(1, 1)
 
@@ -107,16 +107,27 @@ def tile_picked_cbn_none_po_kernel(tc, x_words, x_scales, w1, gamma, beta, offs,
             load_beta(t, 4 + t)
 
         acc = [psum.tile([P, S], F32, name=f"acc{t}") for t in range(PACK)]
-        for t in range(PACK):
+        first = psum.tile([P, QUARTER], F32, name="first")
+
+        def multiply(out, t, lo, hi):
             nc.tensor.matmul_mx(
-                out=acc[t][:],
+                out=out,
                 lhsT=w_codes[:, t * P : (t + 1) * P].bitcast(FP8X4),
                 lhsT_scale=w_scales[:, t * P : (t + 1) * P],
-                rhs=picked_words[:].bitcast(FP8X4),
-                rhs_scale=picked_scales[:],
+                rhs=picked_words[:, lo:hi].bitcast(FP8X4),
+                rhs_scale=picked_scales[:, lo:hi],
                 start=True,
                 stop=True,
             )
+
+        multiply(first[:], 0, S - QUARTER, S)
+        multiply(acc[0][:, 0:HALF], 0, 0, HALF)
+        multiply(acc[0][:, HALF : S - QUARTER], 0, HALF, S - QUARTER)
+        for t in range(1, PACK):
+            multiply(acc[t][:], t, 0, S)
+
+        def product(t, lo, hi):
+            return first[:] if (t, hi) == (0, S) else acc[t][:, lo:hi]
 
         scaled = [keep.tile([P, S], F32, name=f"scaled{t}", align_bytes=64) for t in range(PACK)]
         result = keep.tile([P, PACK, S], F32, name="result", align_bytes=DMA_ALIGN)
@@ -130,7 +141,7 @@ def tile_picked_cbn_none_po_kernel(tc, x_words, x_scales, w1, gamma, beta, offs,
                 look_up(picked_gamma[:, lo:hi], gamma_table[t], lo, hi)
             nc.vector.tensor_copy(out=picked_gamma[:, own[0] : own[1]], in_=gamma_table[t][:].indirect(entries(cls_t, *own)))
             for lo, hi in (others[0], own, *others[1:]):
-                nc.vector.tensor_tensor(out=scaled[t][:, lo:hi], in0=acc[t][:, lo:hi], in1=picked_gamma[:, lo:hi], op=MULT)
+                nc.vector.tensor_tensor(out=scaled[t][:, lo:hi], in0=product(t, lo, hi), in1=picked_gamma[:, lo:hi], op=MULT)
 
         picked_beta = [keep.tile([P, HALF], F32, name=f"picked_beta{t}", align_bytes=64) for t in range(PACK)]
 

@@ -32,9 +32,11 @@ SCALE_OFFSET = TABLE_BYTES - T // 2
 W_OFFSET = 2 * TABLE_BYTES + TABLE_BYTES // 2
 X_OFFSET = 5 * TABLE_BYTES + TABLE_BYTES // 2
 W_SPLIT = 48
+LAST_PIECE = 104
 THREE_QUARTERS = ((0, S - QUARTER), (S - QUARTER, S))
 BY_HALVES = ((0, HALF), (HALF, S))
 ONE_QUARTER = ((0, QUARTER), (QUARTER, QUARTER + HALF), (QUARTER + HALF, S))
+BETA_SPLITS = (HALF, HALF, HALF + 32, HALF)
 GAMMA_PARTS = (THREE_QUARTERS, BY_HALVES, BY_HALVES, ONE_QUARTER)
 
 
@@ -149,30 +151,36 @@ def tile_picked_cbn_none_po_kernel(tc, x_words, x_scales, w1, gamma, beta, offs,
             nc.vector.tensor_tensor(out=result[:, t, lo:hi], in0=beta_table[t][:].indirect(entries(cls_t, lo, hi)), in1=scaled[t][:, lo:hi], op=ADD)
 
         def add_picked(t):
-            nc.vector.tensor_tensor(out=result[:, t, HALF:S], in0=picked_beta[t][:], in1=scaled[t][:, HALF:S], op=ADD)
+            split = BETA_SPLITS[t]
+            nc.vector.tensor_tensor(out=result[:, t, split:S], in0=picked_beta[t][:, 0 : S - split], in1=scaled[t][:, split:S], op=ADD)
 
         for t in range(LAST):
-            look_up(picked_beta[t][:], beta_table[t], HALF, S)
-            add_fused(t, 0, HALF)
+            split = BETA_SPLITS[t]
+            look_up(picked_beta[t][:, 0 : S - split], beta_table[t], split, S)
+            add_fused(t, 0, split)
             add_picked(t)
             if t == 1:
                 nc.sync.dma_start(out=out_slots[:, 0:2, :], in_=result[:, 0:2, :])
         nc.sync.dma_start(out=out_slots[:, 2, :], in_=result[:, 2, :])
 
-        rounded = [keep.tile([P, QUARTER, PACK], BF16, name=f"rounded{q}", align_bytes=64) for q in range(S // QUARTER)]
+        rounded = {lo: keep.tile([P, hi - lo, PACK], BF16, name=f"rounded{lo}", align_bytes=64) for lo, hi in ((0, QUARTER), (QUARTER, HALF), (HALF, S))}
         out_codes = keep.tile([P, S], I32, name="out_codes", align_bytes=DMA_ALIGN)
         out_scales = keep.tile([P, S], U8, name="out_scales", align_bytes=DMA_ALIGN)
         out_words = out_1[0].rearrange("p c r -> p (c r)").bitcast(I32)
 
-        def round_quarter(copy, q):
+        def rounded_part(lo, hi):
+            start = max(first for first in rounded if first <= lo)
+            return rounded[start][:, lo - start : hi - start]
+
+        def round_entries(copy, lo, hi):
             copy(
-                out=rounded[q][:].rearrange("p (c i) t -> p c t i", i=PACK),
-                in_=result[:, :, q * QUARTER : (q + 1) * QUARTER].rearrange("p t (c i) -> p c t i", i=PACK),
+                out=rounded_part(lo, hi).rearrange("p (c i) t -> p c t i", i=PACK),
+                in_=result[:, :, lo:hi].rearrange("p t (c i) -> p c t i", i=PACK),
             )
 
         def quantise(q):
-            columns = slice(q * QUARTER, (q + 1) * QUARTER)
-            nc.vector.quantize_mx(out=out_codes[:, columns].bitcast(FP8X4), scales=out_scales[:, columns], in_=rounded[q][:].rearrange("p c t -> p (c t)"))
+            lo, hi = q * QUARTER, (q + 1) * QUARTER
+            nc.vector.quantize_mx(out=out_codes[:, lo:hi].bitcast(FP8X4), scales=out_scales[:, lo:hi], in_=rounded_part(lo, hi).rearrange("p c t -> p (c t)"))
 
         def store_words(lo, hi):
             nc.sync.dma_start(out=out_words[:, lo:hi], in_=out_codes[:, lo:hi])
@@ -180,13 +188,13 @@ def tile_picked_cbn_none_po_kernel(tc, x_words, x_scales, w1, gamma, beta, offs,
         look_up(picked_beta[LAST][:], beta_table[LAST], HALF, S)
         add_fused(LAST, 0, QUARTER)
         add_fused(LAST, QUARTER, HALF)
-        round_quarter(nc.vector.tensor_copy, 0)
-        round_quarter(nc.scalar.copy, 1)
+        round_entries(nc.vector.tensor_copy, 0, QUARTER)
+        round_entries(nc.scalar.copy, QUARTER, HALF)
         add_picked(LAST)
         nc.sync.dma_start(out=out_slots[:, LAST, :], in_=result[:, LAST, :])
         quantise(0)
-        round_quarter(nc.vector.tensor_copy, 2)
-        round_quarter(nc.scalar.copy, 3)
+        round_entries(nc.vector.tensor_copy, HALF, S - LAST_PIECE)
+        round_entries(nc.scalar.copy, S - LAST_PIECE, S)
         quantise(1)
         store_words(0, HALF)
         quantise(2)

@@ -37,7 +37,8 @@ THREE_QUARTERS = ((0, S - QUARTER), (S - QUARTER, S))
 BY_HALVES = ((0, HALF), (HALF, S))
 ONE_QUARTER = ((0, QUARTER), (QUARTER, QUARTER + HALF), (QUARTER + HALF, S))
 BETA_SPLITS = (HALF, HALF, HALF + 32, HALF)
-GAMMA_PARTS = (THREE_QUARTERS, BY_HALVES, BY_HALVES, ONE_QUARTER)
+HALF_AND_QUARTERS = ((0, HALF), (HALF, S - QUARTER), (S - QUARTER, S))
+GAMMA_PARTS = (HALF_AND_QUARTERS, BY_HALVES, BY_HALVES, ONE_QUARTER)
 
 
 def tile_picked_cbn_none_po_kernel(tc, x_words, x_scales, w1, gamma, beta, offs, cls, out_0, out_1, out_2):
@@ -66,7 +67,7 @@ def tile_picked_cbn_none_po_kernel(tc, x_words, x_scales, w1, gamma, beta, offs,
 
         nc.scalar.dma_start(out=x_scale_table[LANDING : 2 * QUADRANT, :].bitcast(I32), in_=x_scales[0].bitcast(I32))
         for lo, hi in ((0, LANDING), (2 * QUADRANT, P)):
-            nc.vector.memset(x_scale_table[lo:hi, :].bitcast(I32), 0)
+            nc.gpsimd.memset(x_scale_table[lo:hi, :].bitcast(I32), 0)
         picked_scales = keep.tile([P, S], U8, name="picked_scales", align_bytes=64)
         nc.vector.memset(picked_scales[:].bitcast(I32), 0)
 
@@ -104,12 +105,13 @@ def tile_picked_cbn_none_po_kernel(tc, x_words, x_scales, w1, gamma, beta, offs,
         nc.vector.quantize_mx(out=w_codes[:].bitcast(FP8X4), scales=w_scales[:], in_=w_bf[:].rearrange("p t m r -> p (t m r)"))
 
         picked_words = keep.tile([P, S], U32, name="picked_words", tag="w_bf_then_picked_words", align_bytes=64)
-        nc.vector.tensor_copy(out=picked_words[:], in_=x_word_table[:].bitcast(U32).indirect(offs_t[:]))
+        for lo, hi in THREE_QUARTERS:
+            nc.vector.tensor_copy(out=picked_words[:, lo:hi], in_=x_word_table[:].bitcast(U32).indirect(entries(offs_t, lo, hi)))
         for t in (1, 2, 3):
             load_beta(t, 4 + t)
 
         acc = [psum.tile([P, S], F32, name=f"acc{t}") for t in range(PACK)]
-        first = psum.tile([P, QUARTER], F32, name="first")
+        first = {lo: psum.tile([P, QUARTER], F32, name=f"first{lo}") for lo in (HALF, S - QUARTER)}
 
         def multiply(out, t, lo, hi):
             nc.tensor.matmul_mx(
@@ -122,14 +124,14 @@ def tile_picked_cbn_none_po_kernel(tc, x_words, x_scales, w1, gamma, beta, offs,
                 stop=True,
             )
 
-        multiply(first[:], 0, S - QUARTER, S)
+        multiply(first[HALF][:], 0, HALF, S - QUARTER)
         multiply(acc[0][:, 0:HALF], 0, 0, HALF)
-        multiply(acc[0][:, HALF : S - QUARTER], 0, HALF, S - QUARTER)
+        multiply(first[S - QUARTER][:], 0, S - QUARTER, S)
         for t in range(1, PACK):
             multiply(acc[t][:], t, 0, S)
 
         def product(t, lo, hi):
-            return first[:] if (t, hi) == (0, S) else acc[t][:, lo:hi]
+            return first[lo][:] if t == 0 and lo in first else acc[t][:, lo:hi]
 
         scaled = [keep.tile([P, S], F32, name=f"scaled{t}", align_bytes=64) for t in range(PACK)]
         result = keep.tile([P, PACK, S], F32, name="result", align_bytes=DMA_ALIGN)

@@ -32,11 +32,11 @@ SCALE_OFFSET = TABLE_BYTES - T // 2
 W_OFFSET = 2 * TABLE_BYTES + TABLE_BYTES // 2
 X_OFFSET = 5 * TABLE_BYTES + TABLE_BYTES // 2
 W_SPLIT = 48
-LAST_PIECE = 104
+FIRST_PIECE, LAST_SPLIT, LAST_PIECE = QUARTER, HALF + 64, S - QUARTER
 THREE_QUARTERS = ((0, S - QUARTER), (S - QUARTER, S))
 BY_HALVES = ((0, HALF), (HALF, S))
 ONE_QUARTER = ((0, QUARTER), (QUARTER, QUARTER + HALF), (QUARTER + HALF, S))
-BETA_SPLITS = (HALF, HALF, HALF + 32, HALF)
+BETA_SPLITS = (HALF, HALF, HALF + 32, LAST_SPLIT)
 HALF_AND_QUARTERS = ((0, HALF), (HALF, S - QUARTER), (S - QUARTER, S))
 GAMMA_PARTS = (HALF_AND_QUARTERS, BY_HALVES, BY_HALVES, ONE_QUARTER)
 
@@ -65,11 +65,11 @@ def tile_picked_cbn_none_po_kernel(tc, x_words, x_scales, w1, gamma, beta, offs,
         beta_slots = beta.rearrange("(p t) u -> p t u", t=PACK)
         out_slots = out_0.rearrange("(p t) s -> p t s", t=PACK)
 
+        picked_scales = keep.tile([P, S], U8, name="picked_scales", align_bytes=64)
+        nc.gpsimd.memset(picked_scales[:].bitcast(I32), 0)
         nc.scalar.dma_start(out=x_scale_table[LANDING : 2 * QUADRANT, :].bitcast(I32), in_=x_scales[0].bitcast(I32))
         for lo, hi in ((0, LANDING), (2 * QUADRANT, P)):
             nc.gpsimd.memset(x_scale_table[lo:hi, :].bitcast(I32), 0)
-        picked_scales = keep.tile([P, S], U8, name="picked_scales", align_bytes=64)
-        nc.vector.memset(picked_scales[:].bitcast(I32), 0)
 
         nc.sync.dma_start(out=offs_t[:], in_=offs)
         nc.sync.dma_start(out=w_raw[:], in_=w1.rearrange("(p r) c -> p r c", r=PACK))
@@ -165,7 +165,11 @@ def tile_picked_cbn_none_po_kernel(tc, x_words, x_scales, w1, gamma, beta, offs,
                 nc.sync.dma_start(out=out_slots[:, 0:2, :], in_=result[:, 0:2, :])
         nc.sync.dma_start(out=out_slots[:, 2, :], in_=result[:, 2, :])
 
-        rounded = {lo: keep.tile([P, hi - lo, PACK], BF16, name=f"rounded{lo}", align_bytes=64) for lo, hi in ((0, QUARTER), (QUARTER, HALF), (HALF, S))}
+        rounded = {
+            0: keep.tile([P, FIRST_PIECE, PACK], BF16, name="rounded_first", align_bytes=64),
+            FIRST_PIECE: shared.tile([P, LAST_PIECE - FIRST_PIECE, PACK], BF16, name="rounded_middle", align_bytes=DMA_ALIGN, offset=(2 * PACK - 1) * TABLE_BYTES),
+            LAST_PIECE: keep.tile([P, S - LAST_PIECE, PACK], BF16, name="rounded_last", align_bytes=64),
+        }
         out_codes = keep.tile([P, S], I32, name="out_codes", align_bytes=DMA_ALIGN)
         out_scales = keep.tile([P, S], U8, name="out_scales", align_bytes=DMA_ALIGN)
         out_words = out_1[0].rearrange("p c r -> p (c r)").bitcast(I32)
@@ -187,16 +191,16 @@ def tile_picked_cbn_none_po_kernel(tc, x_words, x_scales, w1, gamma, beta, offs,
         def store_words(lo, hi):
             nc.sync.dma_start(out=out_words[:, lo:hi], in_=out_codes[:, lo:hi])
 
-        look_up(picked_beta[LAST][:], beta_table[LAST], HALF, S)
-        add_fused(LAST, 0, QUARTER)
-        add_fused(LAST, QUARTER, HALF)
-        round_entries(nc.vector.tensor_copy, 0, QUARTER)
-        round_entries(nc.scalar.copy, QUARTER, HALF)
+        look_up(picked_beta[LAST][:, 0 : S - LAST_SPLIT], beta_table[LAST], LAST_SPLIT, S)
+        add_fused(LAST, 0, FIRST_PIECE)
+        add_fused(LAST, FIRST_PIECE, LAST_SPLIT)
+        round_entries(nc.scalar.copy, 0, FIRST_PIECE)
         add_picked(LAST)
         nc.sync.dma_start(out=out_slots[:, LAST, :], in_=result[:, LAST, :])
+        round_entries(nc.scalar.copy, LAST_PIECE, S)
+        round_entries(nc.vector.tensor_copy, FIRST_PIECE, LAST_SPLIT)
+        round_entries(nc.vector.tensor_copy, LAST_SPLIT, LAST_PIECE)
         quantise(0)
-        round_entries(nc.vector.tensor_copy, HALF, S - LAST_PIECE)
-        round_entries(nc.scalar.copy, S - LAST_PIECE, S)
         quantise(1)
         store_words(0, HALF)
         quantise(2)

@@ -200,13 +200,12 @@ def tile_picked_cbn_none_po_kernel(tc, x_words, x_scales, w1, gamma, beta, offs,
         round_entries(nc.scalar.copy, LAST_PIECE, S)
         round_entries(nc.vector.tensor_copy, FIRST_PIECE, LAST_SPLIT)
         round_entries(nc.vector.tensor_copy, LAST_SPLIT, LAST_PIECE)
-        quantise(0)
-        quantise(1)
-        store_words(0, HALF)
+        for q in (0, 1):
+            quantise(q)
+            store_words(q * QUARTER, (q + 1) * QUARTER)
         quantise(2)
-        store_words(HALF, S - QUARTER)
         quantise(3)
-        store_words(S - QUARTER, S)
+        store_words(HALF, S)
 
         for q in range(QUADRANTS):
             queue = nc.scalar if q % 2 == 0 else nc.sync

from contextlib import ExitStack

import concourse.mybir as mybir

K, T, S, N, U = 512, 2048, 512, 512, 1024
FLOPS = 2 * K * N * S

F32 = mybir.dt.float32
BF16 = mybir.dt.bfloat16
I32 = mybir.dt.int32
U32 = mybir.dt.uint32
U16 = mybir.dt.uint16
U8 = mybir.dt.uint8
FP8X4 = mybir.dt.float8_e4m3fn_x4
MULT = mybir.AluOpType.mult
ADD = mybir.AluOpType.add
COPY = mybir.ActivationFunctionType.Copy

P = 128
PACK = 4
QUADRANT = 32
SCALE_ROWS = 4
QUADRANTS = P // QUADRANT
LIST_ROWS = 16
HALF = S // 2
QUARTER = S // 4
LAST = PACK - 1
LANDING = 48
DMA_ALIGN = 256
TABLE_BYTES = 4 * U
SCALE_OFFSET = TABLE_BYTES - T // 2
W_OFFSET = 2 * TABLE_BYTES + TABLE_BYTES // 2
X_OFFSET = 5 * TABLE_BYTES + TABLE_BYTES // 2
W_SPLIT = 48
FIRST_PIECE, LAST_SPLIT, LAST_PIECE = QUARTER, HALF + 64, S - QUARTER
THREE_QUARTERS = ((0, S - QUARTER), (S - QUARTER, S))
BY_HALVES = ((0, HALF), (HALF, S))
ONE_QUARTER = ((0, QUARTER), (QUARTER, QUARTER + HALF), (QUARTER + HALF, S))
BETA_SPLITS = (HALF, HALF, HALF + 32, LAST_SPLIT)
HALF_AND_QUARTERS = ((0, HALF), (HALF, S - QUARTER), (S - QUARTER, S))
GAMMA_PARTS = (HALF_AND_QUARTERS, BY_HALVES, BY_HALVES, ONE_QUARTER)


def tile_picked_cbn_none_po_kernel(tc, x_words, x_scales, w1, gamma, beta, offs, cls, out_0, out_1, out_2):
    nc = tc.nc
    with ExitStack() as ctx:
        keep = ctx.enter_context(tc.tile_pool(name="keep", bufs=1))
        shared = ctx.enter_context(tc.tile_pool(name="tables", bufs=1))
        psum = ctx.enter_context(tc.psum_pool(name="psum", bufs=1))

        def entries(list_tile, lo, hi):
            return list_tile[:, lo // LIST_ROWS : hi // LIST_ROWS]

        def scale_rows(tile, q):
            return tile[QUADRANT * q : QUADRANT * q + SCALE_ROWS, :]

        offs_t = keep.tile([P, S // LIST_ROWS], U16, name="offs_t")
        cls_t = keep.tile([P, S // LIST_ROWS], U16, name="cls_t")
        x_word_table = shared.tile([P, T], I32, name="x_word_table", align_bytes=DMA_ALIGN, offset=X_OFFSET)
        x_scale_table = shared.tile([P, T], U8, name="x_scale_table", align_bytes=DMA_ALIGN, offset=SCALE_OFFSET)
        w_raw = shared.tile([P, PACK, N], F32, name="w_raw", align_bytes=DMA_ALIGN, offset=W_OFFSET)
        gamma_table, beta_table = {}, {}

        gamma_slots = gamma.rearrange("(p t) u -> p t u", t=PACK)
        beta_slots = beta.rearrange("(p t) u -> p t u", t=PACK)
        out_slots = out_0.rearrange("(p t) s -> p t s", t=PACK)

        picked_scales = keep.tile([P, S], U8, name="picked_scales", align_bytes=64)
        nc.gpsimd.memset(picked_scales[:].bitcast(I32), 0)
        nc.scalar.dma_start(out=x_scale_table[LANDING : 2 * QUADRANT, :].bitcast(I32), in_=x_scales[0].bitcast(I32))
        for lo, hi in ((0, LANDING), (2 * QUADRANT, P)):
            nc.gpsimd.memset(x_scale_table[lo:hi, :].bitcast(I32), 0)

        nc.sync.dma_start(out=offs_t[:], in_=offs)
        nc.sync.dma_start(out=w_raw[:], in_=w1.rearrange("(p r) c -> p r c", r=PACK))
        nc.sync.dma_start(out=x_word_table[:], in_=x_words[0].rearrange("p c r -> p (c r)").bitcast(I32))
        nc.sync.dma_start(out=cls_t[:], in_=cls)

        def load_gamma(t, place):
            gamma_table[t] = shared.tile([P, U], F32, name=f"gamma_table{t}", align_bytes=DMA_ALIGN, offset=place * TABLE_BYTES)
            nc.sync.dma_start(out=gamma_table[t][:], in_=gamma_slots[:, t, :])

        def load_beta(t, place):
            beta_table[t] = shared.tile([P, U], F32, name=f"beta_table{t}", align_bytes=DMA_ALIGN, offset=place * TABLE_BYTES)
            nc.sync.dma_start(out=beta_table[t][:], in_=beta_slots[:, t, :])

        w_bf = keep.tile([P, PACK, P, PACK], BF16, name="w_bf", tag="w_bf_then_picked_words", align_bytes=64)
        w_dst = w_bf[:].rearrange("p t m r -> p m r t")
        w_src = w_raw[:].rearrange("p r (m t) -> p m r t", t=PACK)
        nc.scalar.copy(out=w_dst[:, 0:W_SPLIT], in_=w_src[:, 0:W_SPLIT])

        picked_landing = keep.tile([P, S], U8, name="picked_landing", align_bytes=64)
        nc.vector.tensor_copy(out=picked_landing[:], in_=x_scale_table[:].indirect(offs_t[:]))
        for r in range(SCALE_ROWS):
            nc.sync.dma_start(out=picked_scales[r:P:QUADRANT, :].bitcast(I32), in_=picked_landing[LANDING + r : 2 * QUADRANT : SCALE_ROWS, :].bitcast(I32))
        load_gamma(0, 0)
        load_gamma(1, 1)

        nc.vector.tensor_copy(out=w_dst[:, W_SPLIT:P], in_=w_src[:, W_SPLIT:P])
        load_gamma(2, 2)
        load_gamma(3, 3)
        load_beta(0, 4)
        w_codes = keep.tile([P, N], U32, name="w_codes", align_bytes=64)
        w_scales = keep.tile([P, N], U8, name="w_scales", align_bytes=64)
        nc.vector.quantize_mx(out=w_codes[:].bitcast(FP8X4), scales=w_scales[:], in_=w_bf[:].rearrange("p t m r -> p (t m r)"))

        picked_words = keep.tile([P, S], U32, name="picked_words", tag="w_bf_then_picked_words", align_bytes=64)
        for lo, hi in THREE_QUARTERS:
            nc.vector.tensor_copy(out=picked_words[:, lo:hi], in_=x_word_table[:].bitcast(U32).indirect(entries(offs_t, lo, hi)))
        for t in (1, 2, 3):
            load_beta(t, 4 + t)

        acc = [psum.tile([P, S], F32, name=f"acc{t}") for t in range(PACK)]
        first = {lo: psum.tile([P, QUARTER], F32, name=f"first{lo}") for lo in (HALF, S - QUARTER)}

        def multiply(out, t, lo, hi):
            nc.tensor.matmul_mx(
                out=out,
                lhsT=w_codes[:, t * P : (t + 1) * P].bitcast(FP8X4),
                lhsT_scale=w_scales[:, t * P : (t + 1) * P],
                rhs=picked_words[:, lo:hi].bitcast(FP8X4),
                rhs_scale=picked_scales[:, lo:hi],
                start=True,
                stop=True,
            )

        multiply(first[HALF][:], 0, HALF, S - QUARTER)
        multiply(acc[0][:, 0:HALF], 0, 0, HALF)
        multiply(first[S - QUARTER][:], 0, S - QUARTER, S)
        for t in range(1, PACK):
            multiply(acc[t][:], t, 0, S)

        def product(t, lo, hi):
            return first[lo][:] if t == 0 and lo in first else acc[t][:, lo:hi]

        scaled = [keep.tile([P, S], F32, name=f"scaled{t}", align_bytes=64) for t in range(PACK)]
        result = keep.tile([P, PACK, S], F32, name="result", align_bytes=DMA_ALIGN)

        def look_up(picked, table, lo, hi):
            nc.scalar.activation(out=picked, in_=table[:].indirect(entries(cls_t, lo, hi)), func=COPY)

        for t, (own, *others) in enumerate(GAMMA_PARTS):
            picked_gamma = keep.tile([P, S], F32, name=f"picked_gamma{t}", align_bytes=64)
            for lo, hi in others:
                look_up(picked_gamma[:, lo:hi], gamma_table[t], lo, hi)
            nc.vector.tensor_copy(out=picked_gamma[:, own[0] : own[1]], in_=gamma_table[t][:].indirect(entries(cls_t, *own)))
            for lo, hi in (others[0], own, *others[1:]):
                nc.vector.tensor_tensor(out=scaled[t][:, lo:hi], in0=product(t, lo, hi), in1=picked_gamma[:, lo:hi], op=MULT)

        picked_beta = [keep.tile([P, HALF], F32, name=f"picked_beta{t}", align_bytes=64) for t in range(PACK)]

        def add_fused(t, lo, hi):
            nc.vector.tensor_tensor(out=result[:, t, lo:hi], in0=beta_table[t][:].indirect(entries(cls_t, lo, hi)), in1=scaled[t][:, lo:hi], op=ADD)

        def add_picked(t):
            split = BETA_SPLITS[t]
            nc.vector.tensor_tensor(out=result[:, t, split:S], in0=picked_beta[t][:, 0 : S - split], in1=scaled[t][:, split:S], op=ADD)

        for t in range(LAST):
            split = BETA_SPLITS[t]
            look_up(picked_beta[t][:, 0 : S - split], beta_table[t], split, S)
            add_fused(t, 0, split)
            add_picked(t)
            if t == 1:
                nc.sync.dma_start(out=out_slots[:, 0:2, :], in_=result[:, 0:2, :])
        nc.sync.dma_start(out=out_slots[:, 2, :], in_=result[:, 2, :])

        rounded = {
            0: keep.tile([P, FIRST_PIECE, PACK], BF16, name="rounded_first", align_bytes=64),
            FIRST_PIECE: shared.tile([P, LAST_PIECE - FIRST_PIECE, PACK], BF16, name="rounded_middle", align_bytes=DMA_ALIGN, offset=(2 * PACK - 1) * TABLE_BYTES),
            LAST_PIECE: keep.tile([P, S - LAST_PIECE, PACK], BF16, name="rounded_last", align_bytes=64),
        }
        out_codes = keep.tile([P, S], I32, name="out_codes", align_bytes=DMA_ALIGN)
        out_scales = keep.tile([P, S], U8, name="out_scales", align_bytes=DMA_ALIGN)
        out_words = out_1[0].rearrange("p c r -> p (c r)").bitcast(I32)

        def rounded_part(lo, hi):
            start = max(first for first in rounded if first <= lo)
            return rounded[start][:, lo - start : hi - start]

        def round_entries(copy, lo, hi):
            copy(
                out=rounded_part(lo, hi).rearrange("p (c i) t -> p c t i", i=PACK),
                in_=result[:, :, lo:hi].rearrange("p t (c i) -> p c t i", i=PACK),
            )

        def quantise(q):
            lo, hi = q * QUARTER, (q + 1) * QUARTER
            nc.vector.quantize_mx(out=out_codes[:, lo:hi].bitcast(FP8X4), scales=out_scales[:, lo:hi], in_=rounded_part(lo, hi).rearrange("p c t -> p (c t)"))

        def store_words(lo, hi):
            nc.sync.dma_start(out=out_words[:, lo:hi], in_=out_codes[:, lo:hi])

        look_up(picked_beta[LAST][:, 0 : S - LAST_SPLIT], beta_table[LAST], LAST_SPLIT, S)
        add_fused(LAST, 0, FIRST_PIECE)
        add_fused(LAST, FIRST_PIECE, LAST_SPLIT)
        round_entries(nc.scalar.copy, 0, FIRST_PIECE)
        add_picked(LAST)
        nc.sync.dma_start(out=out_slots[:, LAST, :], in_=result[:, LAST, :])
        round_entries(nc.scalar.copy, LAST_PIECE, S)
        round_entries(nc.vector.tensor_copy, FIRST_PIECE, LAST_SPLIT)
        round_entries(nc.vector.tensor_copy, LAST_SPLIT, LAST_PIECE)
        for q in (0, 1):
            quantise(q)
            store_words(q * QUARTER, (q + 1) * QUARTER)
        quantise(2)
        quantise(3)
        store_words(HALF, S)

        for q in range(QUADRANTS):
            queue = nc.scalar if q % 2 == 0 else nc.sync
            queue.dma_start(out=out_2[0, SCALE_ROWS * q : SCALE_ROWS * (q + 1), :].bitcast(I32), in_=scale_rows(out_scales, q).bitcast(I32))
